import numpy as np
import ml_dtypes


def mxq(x, axis, fmt="e4m3"):
    dtype, down = {"e4m3": (ml_dtypes.float8_e4m3fn, 7), "e5m2": (ml_dtypes.float8_e5m2, 14)}[fmt]
    v = np.moveaxis(np.asarray(x, np.float32).astype(ml_dtypes.bfloat16).astype(np.float64), axis, -1)
    blocks = v.reshape(v.shape[:-1] + (-1, 32))
    amax = np.abs(blocks).max(-1, keepdims=True)
    byte = np.maximum(np.where(amax > 0, np.frexp(amax)[1] - 1 + 127, 0) - down, 1)
    scale = np.exp2(byte - 127.0)
    codes = (blocks / scale).astype(np.float32).astype(dtype).astype(np.float64)
    return np.moveaxis((codes * scale).reshape(v.shape), -1, axis)


WIDE = False


def mx_kscale(k):
    if not WIDE:
        return np.ones(k)
    levels = np.array([18, -18])
    if k % 512:
        return np.exp2(np.random.permutation(np.resize(levels, k // 32))).repeat(32)
    a = np.empty((k // 512, 16))
    for p in range(k // 512):
        a[p, :8] = np.random.permutation(np.resize(levels, 8))
        for g in range(8):
            far = levels[np.abs(levels - a[p, g]) >= 10]
            a[p, g + 8] = far[np.random.randint(len(far))]
    return np.exp2(a.ravel()).repeat(32)


def f64(x):
    return np.asarray(x).astype(np.float64)


def striped(idx):
    return np.tile(np.asarray(idx).reshape(-1, 16).T, (8, 1)).astype(np.uint16)


def unstriped(offs):
    return offs[:16].T.reshape(-1).astype(np.int64)


def setup_inputs():
    n = np.random.standard_normal
    uni = np.random.uniform
    idx = np.random.permutation(2048)[:512]
    f_d = mx_kscale(512)
    f_e = mx_kscale(512)
    f_i = np.ones(2048)
    f_i[idx] = mx_kscale(512)
    return {
        "xT": (n((512, 512)) * f_d[:, None] * f_i[idx][None, :]).astype(np.float32),
        "dz": (n((512, 512))).astype(np.float32),
        "cf": (uni(0.75, 1.3, (512, 1))).astype(np.float32),
        "si": np.tile(uni(0.75, 1.3, 512), (128, 1)).astype(np.float32),
        "U": (n((512, 512)) / np.sqrt(512) / f_d[:, None]).astype(np.float32),
        "eT": (n((512, 2048)) * f_e[:, None] / f_i[None, :]).astype(np.float32),
        "V": (n((512, 512)) / np.sqrt(512) / f_e[:, None]).astype(np.float32),
        "offs": striped(idx),
    }


def reference(xT, dz, cf, si, U, eT, V, offs):
    idx = unstriped(offs)
    eT_i = f64(eT)[:, idx]
    u = mxq(f64(U), 0, "e4m3").T @ mxq(f64(xT), 0, "e4m3")
    dv = f64(cf) * f64(si)[:1] * f64(dz) * u
    v = mxq(f64(V), 0, "e4m3").T @ mxq(eT_i, 0, "e4m3")
    du = f64(cf) * f64(si)[:1] * f64(dz) * v
    out_0 = mxq(f64(xT), 1, "e4m3") @ mxq(du, 1, "e5m2").T
    out_1 = mxq(eT_i, 1, "e4m3") @ mxq(dv, 1, "e5m2").T
    return out_0, out_1

@@ -1,0 +1,231 @@
+from contextlib import ExitStack
+
+import concourse.mybir as mybir
+
+F32 = mybir.dt.float32
+BF16 = mybir.dt.bfloat16
+U32 = mybir.dt.uint32
+U16 = mybir.dt.uint16
+U8 = mybir.dt.uint8
+E4M3 = mybir.dt.float8_e4m3fn_x4
+E5M2 = mybir.dt.float8_e5m2_x4
+MULT = mybir.AluOpType.mult
+
+P = 128
+PACK = 4
+K = 512
+ITEMS = 2048
+FLOPS = 4 * 2 * K * K * K
+
+
+def tile_attend_gbpool_UV_kernel(tc, xT, dz, cf, si, U, eT, V, offs, out_0, out_1):
+    nc = tc.nc
+    with ExitStack() as ctx:
+        keep = ctx.enter_context(tc.tile_pool(name="keep", bufs=1))
+        psum = ctx.enter_context(tc.psum_pool(name="psum", bufs=8))
+
+        def sb(name, shape, dtype, tag=None):
+            return keep.tile(shape, dtype, name=name, tag=tag or name, align_bytes=64)
+
+        def new_bank(shape):
+            return psum.tile(shape, F32, name="bank")
+
+        def load_halves(name, src):
+            rows = src.rearrange("(p t) c -> p t c", t=PACK)
+            halves = []
+            for a in range(2):
+                half = sb("%s_raw%d" % (name, a), [P, PACK, K // 2], F32)
+                nc.sync.dma_start(out=half[:], in_=rows[:, :, a * (K // 2):(a + 1) * (K // 2)])
+                halves.append(half)
+            return halves
+
+        si_col = sb("si_col", [P, PACK], F32)
+        nc.sync.dma_start(out=si_col[:], in_=si[0:1, :].rearrange("o (m r) -> m (o r)", r=PACK))
+        cf_col = sb("cf_col", [P, PACK], F32)
+        nc.sync.dma_start(out=cf_col[:], in_=cf.rearrange("(p j) o -> p (j o)", j=PACK))
+        dz_rows = dz.rearrange("(p j) i -> p j i", j=PACK)
+        dz_raw = []
+        for a in range(2):
+            pair = sb("dz_raw%d" % a, [P, 2, K], F32)
+            nc.sync.dma_start(out=pair[:], in_=dz_rows[:, 2 * a:2 * a + 2, :])
+            dz_raw.extend([pair[:, 0, :], pair[:, 1, :]])
+        x_raw = load_halves("x", xT)
+        u_raw = load_halves("u", U)
+        offsets = keep.tile([P, K // 16], U16, name="offsets")
+        nc.sync.dma_start(offsets[:], offs)
+        e_rows = eT.rearrange("(p t) c -> p t c", t=PACK)
+        table = []
+        for t in range(PACK):
+            plane = sb("table%d" % t, [P, ITEMS], F32)
+            nc.sync.dma_start(out=plane[:], in_=e_rows[:, t, :])
+            table.append(plane)
+        v_raw = load_halves("v", V)
+
+        ident = sb("ident", [P, P], F32)
+        ones = sb("ones", [P, P], F32)
+        nc.vector.memset(ones[:], 1.0)
+        ramp = sb("ramp", [P, P], F32)
+        nc.vector.tensor_tensor_scan(out=ramp[:], data0=ones[:], data1=ones[:], initial=-1.0, op0=MULT, op1=mybir.AluOpType.add)
+        turned = sb("turned", [P, P], F32)
+        nc.vector.transpose(out=turned[:], in_=ramp[:])
+        for q in range(0, P, 32):
+            nc.vector.tensor_scalar(out=ident[q:q + 32, :], in0=ramp[q:q + 32, :], scalar1=turned[q:q + 32, q:q + 1],
+                                    scalar2=None, op0=mybir.AluOpType.is_equal)
+
+        def mx_tiles(name, width=K, tag=None):
+            return sb(name + "_codes", [P, width], U32, tag), sb(name + "_scales", [P, width], U8)
+
+        def quantize(mx, fmt, src, c, n=1):
+            cols = slice(c * P, (c + n) * P)
+            nc.vector.quantize_mx(out=mx[0][:, cols].bitcast(fmt), scales=mx[1][:, cols], in_=src)
+
+        def chunks(tile, c, n=1):
+            return tile[:, c * K:(c + n) * K]
+
+        def cast_weights(dst, raw, c, n, copy):
+            part = raw[c // 2][:, :, (c % 2) * P:(c % 2 + n) * P]
+            copy(out=dst.rearrange("p (a b t) -> p a t b", b=4, t=PACK),
+                 in_=part.rearrange("p t (a b) -> p a t b", b=4))
+
+        def project(c, act_mx, w_mx):
+            bank = new_bank([P, PACK, P])
+            cols = slice(c * P, (c + 1) * P)
+            for r in range(PACK):
+                rc = slice(r * P, (r + 1) * P)
+                nc.tensor.matmul_mx(out=bank[:, r, :], lhsT=act_mx[0][:, rc].bitcast(E4M3), lhsT_scale=act_mx[1][:, rc],
+                                    rhs=w_mx[0][:, cols].bitcast(E4M3), rhs_scale=w_mx[1][:, cols],
+                                    start=True, stop=True)
+            return bank
+
+        def weigh(c, bank, wT, dst):
+            nc.vector.tensor_tensor(out=chunks(dst, c).rearrange("p (n r) -> p n r", r=PACK),
+                                    in0=bank[:].rearrange("p r n -> p n r"),
+                                    in1=chunks(wT, c).rearrange("p (n r) -> p n r", r=PACK), op=MULT)
+
+        def turn_pair(src, h):
+            words = src[:].bitcast(F32)
+            bank = new_bank([P, PACK, P])
+            for r in range(PACK):
+                nc.tensor.transpose(bank[:, r, :], words[:, 2 * P * r + h:2 * P * (r + 1):2], ident[:])
+            return bank
+
+        def unturn_pair(bank, dst, h):
+            nc.scalar.copy(out=chunks(dst, 2 * h, 2).rearrange("p (e n r) -> p e n r", e=2, r=PACK),
+                           in_=bank[:].rearrange("p r n -> p (r n)").bitcast(BF16).rearrange("p (r n e) -> p e n r", r=PACK, e=2))
+
+        def turn_planes(src, dst):
+            words = src[:].bitcast(F32)
+            bank = new_bank([P, PACK, P])
+            for e in range(2):
+                for u in range(2):
+                    nc.tensor.transpose(bank[:, 2 * e + u, :], words[:, 2 * P * e + u:2 * P * (e + 1):2], ident[:])
+            nc.scalar.copy(out=dst[:].bitcast(F32).rearrange("p (e n u) -> p e n u", e=2, u=2),
+                           in_=bank[:].rearrange("p (e u) n -> p e n u", u=2))
+
+        def gradient_mm(act_mx, c, d_mx):
+            bank = new_bank([P, K])
+            cols = slice(c * P, (c + 1) * P)
+            nc.tensor.matmul_mx(out=bank[:], lhsT=act_mx[0][:, cols].bitcast(E4M3), lhsT_scale=act_mx[1][:, cols],
+                                rhs=d_mx[0][:].bitcast(E5M2), rhs_scale=d_mx[1][:], start=True, stop=True)
+            return bank
+
+        def store(bank, res, out, t, copy):
+            copy(out=res, in_=bank[:])
+            nc.sync.dma_start(out=out.rearrange("(p t) f -> p t f", t=PACK)[:, t, :], in_=res)
+
+        si_bank = new_bank([P, K])
+        for r in range(PACK):
+            nc.tensor.transpose(si_bank[:, r * P:(r + 1) * P], si_col[:, r:r + 1].to_broadcast([P, P]), ident[:])
+        wT = sb("wT", [P, PACK * K], F32)
+        wT_view = wT[:].rearrange("p (n j r) -> p n j r", j=PACK, r=PACK)
+        for j in range(PACK):
+            w = sb("w%d" % j, [P, K], F32)
+            nc.vector.scalar_tensor_tensor(out=w[:].rearrange("p (r m) -> p m r", r=PACK),
+                                           in0=dz_raw[j].rearrange("p (m r) -> p m r", r=PACK),
+                                           scalar=cf_col[:, j:j + 1],
+                                           in1=si_bank[:].rearrange("p (r m) -> p m r", r=PACK),
+                                           op0=MULT, op1=MULT)
+            bank = new_bank([P, PACK, P])
+            for r in range(PACK):
+                nc.tensor.transpose(bank[:, r, :], w[:, r * P:(r + 1) * P], ident[:])
+            nc.scalar.copy(out=wT_view[:, :, j, :], in_=bank[:].rearrange("p r n -> p n r"))
+
+        x_d = sb("x_d", [P, PACK * K], BF16)
+        x_d_view = x_d[:].rearrange("p (r m t) -> p m t r", r=PACK, t=PACK)
+        for a in range(2):
+            nc.vector.tensor_copy(out=x_d_view[:, a * 64:(a + 1) * 64, :, :],
+                                  in_=x_raw[a][:].rearrange("p t (m r) -> p m t r", r=PACK))
+        xd_mx = mx_tiles("xd")
+        quantize(xd_mx, E4M3, x_d[:], 0, 4)
+
+        x_i = sb("x_i", [P, PACK * K], BF16)
+        x_banks = [turn_pair(x_d, h) for h in range(2)]
+
+        u_b = sb("u_b", [P, PACK * K], BF16)
+        u_mx = mx_tiles("u")
+        dv_b = sb("dv_b", [P, PACK * K], BF16, "u_raw1")
+        dv_mx = mx_tiles("dv")
+        for c in range(2):
+            cast_weights(chunks(u_b, c), u_raw, c, 1, nc.scalar.copy)
+        cast_weights(chunks(u_b, 2, 2), u_raw, 2, 2, nc.vector.tensor_copy)
+        for c in range(2):
+            quantize(u_mx, E4M3, chunks(u_b, c), c)
+        quantize(u_mx, E4M3, chunks(u_b, 2, 2), 2, 2)
+        for h in range(2):
+            unturn_pair(x_banks[h], x_i, h)
+        for c in range(PACK):
+            weigh(c, project(c, xd_mx, u_mx), wT, dv_b)
+        quantize(dv_mx, E5M2, dv_b[:], 0, 4)
+
+        g_e = sb("g_e", [P, PACK * K], BF16)
+        g_e_view = g_e[:].rearrange("p (r m t) -> p m t r", r=PACK, t=PACK)
+        planes = [sb("planes%d" % h, [P, 2 * K], BF16) for h in range(2)]
+
+        def weave(h, copy):
+            copy(out=g_e_view[:, :, 2 * h:2 * h + 2, :],
+                 in_=planes[h][:].rearrange("p (t m r) -> p m t r", t=2, r=PACK))
+
+        for t in range(PACK):
+            nc.vector.tensor_copy(chunks(planes[t // 2], t % 2), table[t][:].indirect(offsets[:]))
+            if t % 2 == 1:
+                weave(t // 2, nc.vector.tensor_copy)
+        g_i0 = sb("g_i0", [P, 2 * K], BF16)
+        turn_planes(planes[0], g_i0)
+        gi_mx = [mx_tiles("gi0", 2 * P, "table2"), mx_tiles("gi1", 2 * P)]
+        quantize(gi_mx[0], E4M3, g_i0[:], 0, 2)
+        early = [gradient_mm(gi_mx[0], t, dv_mx) for t in range(2)]
+
+        v_b = [sb("v_b%d" % c, [P, K], BF16) for c in range(PACK)]
+        for c in range(PACK):
+            cast_weights(v_b[c][:], v_raw, c, 1, nc.scalar.copy)
+        v_mx = mx_tiles("v")
+        quantize(v_mx, E4M3, v_b[0][:], 0)
+        ge_mx = mx_tiles("ge", K, "v_b0")
+        du_b = sb("du_b", [P, PACK * K], BF16)
+        du_mx = mx_tiles("du")
+        for r in range(PACK):
+            quantize(ge_mx, E4M3, chunks(g_e, r), r)
+        g_i1 = sb("g_i1", [P, 2 * K], BF16, tag="v_raw0")
+        turn_planes(planes[1], g_i1)
+        banks = []
+        for c in range(PACK):
+            if c > 0:
+                quantize(v_mx, E4M3, v_b[c][:], c)
+            banks.append(project(c, ge_mx, v_mx))
+        xi_mx = mx_tiles("xi", K, "g_e")
+        quantize(xi_mx, E4M3, x_i[:], 0, 4)
+        quantize(gi_mx[1], E4M3, g_i1[:], 0, 2)
+        res1 = sb("res1", [P, 2, K], F32, "v_raw1")
+        for t in range(2):
+            store(early[t], res1[:, t, :], out_1, t, nc.scalar.copy)
+        for t in range(2, PACK):
+            res = sb("res1_%d" % t, [P, K], F32)
+            store(gradient_mm(gi_mx[1], t - 2, dv_mx), res[:], out_1, t, nc.scalar.copy)
+        for c in range(PACK):
+            weigh(c, banks[c], wT, du_b)
+            if c > 0:
+                quantize(du_mx, E5M2, chunks(du_b, c - 1), c - 1)
+        quantize(du_mx, E5M2, chunks(du_b, PACK - 1), PACK - 1)
+        for t in range(PACK):
+            res = sb("res0_%d" % t, [P, K], F32)
+            store(gradient_mm(xi_mx, t, du_mx), res[:], out_0, t, nc.vector.tensor_copy if t % 2 == 0 else nc.scalar.copy)

@@ -9,12 +9,14 @@ U16 = mybir.dt.uint16
 U8 = mybir.dt.uint8
 E4M3 = mybir.dt.float8_e4m3fn_x4
 E5M2 = mybir.dt.float8_e5m2_x4
-MULT = mybir.AluOpType.mult
+ALU = mybir.AluOpType
 
 P = 128
 PACK = 4
 K = 512
+HALF = K // 2
 ITEMS = 2048
+QUADRANT = 32
 FLOPS = 4 * 2 * K * K * K
 
 
@@ -24,68 +26,56 @@ def tile_attend_gbpool_UV_kernel(tc, xT, dz, cf, si, U, eT, V, offs, out_0, out_
         keep = ctx.enter_context(tc.tile_pool(name="keep", bufs=1))
         psum = ctx.enter_context(tc.psum_pool(name="psum", bufs=8))
 
-        def sb(name, shape, dtype, tag=None):
-            return keep.tile(shape, dtype, name=name, tag=tag or name, align_bytes=64)
+        def sb(name, shape, dtype, slot=None):
+            return keep.tile(shape, dtype, name=name, tag=slot or name, align_bytes=64)
 
         def new_bank(shape):
             return psum.tile(shape, F32, name="bank")
 
-        def load_halves(name, src):
-            rows = src.rearrange("(p t) c -> p t c", t=PACK)
-            halves = []
-            for a in range(2):
-                half = sb("%s_raw%d" % (name, a), [P, PACK, K // 2], F32)
-                nc.sync.dma_start(out=half[:], in_=rows[:, :, a * (K // 2):(a + 1) * (K // 2)])
-                halves.append(half)
-            return halves
+        def chunks(ap, c, n=1):
+            return ap[:, c * K:(c + n) * K]
 
-        si_col = sb("si_col", [P, PACK], F32)
-        nc.sync.dma_start(out=si_col[:], in_=si[0:1, :].rearrange("o (m r) -> m (o r)", r=PACK))
-        cf_col = sb("cf_col", [P, PACK], F32)
-        nc.sync.dma_start(out=cf_col[:], in_=cf.rearrange("(p j) o -> p (j o)", j=PACK))
-        dz_rows = dz.rearrange("(p j) i -> p j i", j=PACK)
-        dz_raw = []
-        for a in range(2):
-            pair = sb("dz_raw%d" % a, [P, 2, K], F32)
-            nc.sync.dma_start(out=pair[:], in_=dz_rows[:, 2 * a:2 * a + 2, :])
-            dz_raw.extend([pair[:, 0, :], pair[:, 1, :]])
-        x_raw = load_halves("x", xT)
-        u_raw = load_halves("u", U)
+        def by_place(dram):
+            return dram.rearrange("(p t) c -> p t c", t=PACK)
+
+        def load(name, src):
+            tile = sb(name, src.shape, F32)
+            nc.sync.dma_start(out=tile[:], in_=src)
+            return tile
+
+        factor_rows = sb("factor_rows", [P, P], F32)
+        nc.vector.memset(factor_rows[:], 0.0)
+        nc.scalar.dma_start(out=factor_rows[0:PACK, :], in_=si[0:1, :].rearrange("o (a m) -> (o a) m", a=PACK))
+        nc.scalar.dma_start(out=factor_rows[PACK:2 * PACK, :], in_=cf.rearrange("(c n) o -> c (n o)", c=PACK))
+        dz_raw = [load("dz_raw%d" % c, dz[c * P:(c + 1) * P, :]) for c in range(PACK)]
+        x_raw = load("x_raw", by_place(xT))
+        u_raw = load("u_raw", by_place(U))
         offsets = keep.tile([P, K // 16], U16, name="offsets")
         nc.sync.dma_start(offsets[:], offs)
-        e_rows = eT.rearrange("(p t) c -> p t c", t=PACK)
-        table = []
-        for t in range(PACK):
-            plane = sb("table%d" % t, [P, ITEMS], F32)
-            nc.sync.dma_start(out=plane[:], in_=e_rows[:, t, :])
-            table.append(plane)
-        v_raw = load_halves("v", V)
+        table = [load("table%d" % t, by_place(eT)[:, t, :]) for t in range(PACK)]
+        v_raw = [load("v_raw%d" % a, by_place(V)[:, :, a * HALF:(a + 1) * HALF]) for a in range(2)]
 
-        ident = sb("ident", [P, P], F32)
         ones = sb("ones", [P, P], F32)
         nc.vector.memset(ones[:], 1.0)
         ramp = sb("ramp", [P, P], F32)
-        nc.vector.tensor_tensor_scan(out=ramp[:], data0=ones[:], data1=ones[:], initial=-1.0, op0=MULT, op1=mybir.AluOpType.add)
-        turned = sb("turned", [P, P], F32)
-        nc.vector.transpose(out=turned[:], in_=ramp[:])
-        for q in range(0, P, 32):
-            nc.vector.tensor_scalar(out=ident[q:q + 32, :], in0=ramp[q:q + 32, :], scalar1=turned[q:q + 32, q:q + 1],
-                                    scalar2=None, op0=mybir.AluOpType.is_equal)
+        nc.vector.tensor_tensor_scan(out=ramp[:], data0=ones[:], data1=ones[:], initial=-1.0, op0=ALU.mult, op1=ALU.add)
+        ramp_turned = sb("ramp_turned", [P, P], F32)
+        nc.vector.transpose(out=ramp_turned[:], in_=ramp[:])
+        ident = sb("ident", [P, P], F32)
+        for q in range(0, P, QUADRANT):
+            rows = slice(q, q + QUADRANT)
+            nc.vector.tensor_scalar(out=ident[rows, :], in0=ramp[rows, :], scalar1=ramp_turned[rows, q:q + 1],
+                                    scalar2=None, op0=ALU.is_equal)
 
-        def mx_tiles(name, width=K, tag=None):
-            return sb(name + "_codes", [P, width], U32, tag), sb(name + "_scales", [P, width], U8)
+        def mx_tiles(name, width, slot=None):
+            return sb(name + "_codes", [P, width], U32, slot), sb(name + "_scales", [P, width], U8)
 
-        def quantize(mx, fmt, src, c, n=1):
-            cols = slice(c * P, (c + n) * P)
+        def quantize(mx, fmt, src, c):
+            cols = slice(c * P, c * P + src.shape[1] // PACK)
             nc.vector.quantize_mx(out=mx[0][:, cols].bitcast(fmt), scales=mx[1][:, cols], in_=src)
 
-        def chunks(tile, c, n=1):
-            return tile[:, c * K:(c + n) * K]
-
-        def cast_weights(dst, raw, c, n, copy):
-            part = raw[c // 2][:, :, (c % 2) * P:(c % 2 + n) * P]
-            copy(out=dst.rearrange("p (a b t) -> p a t b", b=4, t=PACK),
-                 in_=part.rearrange("p t (a b) -> p a t b", b=4))
+        def cast_weights(dst, src, copy):
+            copy(out=dst.rearrange("p (a b t) -> p a t b", b=4, t=PACK), in_=src.rearrange("p t (a b) -> p a t b", b=4))
 
         def project(c, act_mx, w_mx):
             bank = new_bank([P, PACK, P])
@@ -97,135 +87,136 @@ def tile_attend_gbpool_UV_kernel(tc, xT, dz, cf, si, U, eT, V, offs, out_0, out_
                                     start=True, stop=True)
             return bank
 
-        def weigh(c, bank, wT, dst):
-            nc.vector.tensor_tensor(out=chunks(dst, c).rearrange("p (n r) -> p n r", r=PACK),
-                                    in0=bank[:].rearrange("p r n -> p n r"),
-                                    in1=chunks(wT, c).rearrange("p (n r) -> p n r", r=PACK), op=MULT)
-
-        def turn_pair(src, h):
-            words = src[:].bitcast(F32)
-            bank = new_bank([P, PACK, P])
-            for r in range(PACK):
-                nc.tensor.transpose(bank[:, r, :], words[:, 2 * P * r + h:2 * P * (r + 1):2], ident[:])
-            return bank
-
-        def unturn_pair(bank, dst, h):
-            nc.scalar.copy(out=chunks(dst, 2 * h, 2).rearrange("p (e n r) -> p e n r", e=2, r=PACK),
-                           in_=bank[:].rearrange("p r n -> p (r n)").bitcast(BF16).rearrange("p (r n e) -> p e n r", r=PACK, e=2))
+        def weigh(bank, c, dst):
+            nc.vector.tensor_tensor(out=dst.rearrange("p (n r) -> p n r", r=PACK), in0=bank[:].rearrange("p r n -> p n r"),
+                                    in1=chunks(wT, c).rearrange("p (n r) -> p n r", r=PACK), op=ALU.mult)
 
         def turn_planes(src, dst):
-            words = src[:].bitcast(F32)
-            bank = new_bank([P, PACK, P])
-            for e in range(2):
+            n = src.shape[1] // K
+            words = src.bitcast(F32)
+            bank = new_bank([P, 2 * n, P])
+            for e in range(n):
                 for u in range(2):
                     nc.tensor.transpose(bank[:, 2 * e + u, :], words[:, 2 * P * e + u:2 * P * (e + 1):2], ident[:])
-            nc.scalar.copy(out=dst[:].bitcast(F32).rearrange("p (e n u) -> p e n u", e=2, u=2),
+            nc.scalar.copy(out=dst.bitcast(F32).rearrange("p (e n u) -> p e n u", e=n, u=2),
                            in_=bank[:].rearrange("p (e u) n -> p e n u", u=2))
 
-        def gradient_mm(act_mx, c, d_mx):
+        def gradient(act_mx, c, first):
             bank = new_bank([P, K])
             cols = slice(c * P, (c + 1) * P)
+            window = slice(first, first + K)
             nc.tensor.matmul_mx(out=bank[:], lhsT=act_mx[0][:, cols].bitcast(E4M3), lhsT_scale=act_mx[1][:, cols],
-                                rhs=d_mx[0][:].bitcast(E5M2), rhs_scale=d_mx[1][:], start=True, stop=True)
+                                rhs=d_mx[0][:, window].bitcast(E5M2), rhs_scale=d_mx[1][:, window], start=True, stop=True)
             return bank
 
-        def store(bank, res, out, t, copy):
-            copy(out=res, in_=bank[:])
-            nc.sync.dma_start(out=out.rearrange("(p t) f -> p t f", t=PACK)[:, t, :], in_=res)
+        def store_out_1(t, act_mx, c):
+            res = sb("res1_%d" % t, [P, K], F32)
+            nc.scalar.copy(out=res[:], in_=gradient(act_mx, c, 0)[:])
+            nc.sync.dma_start(out=by_place(out_1)[:, t, :], in_=res[:])
 
+        factor_bank = new_bank([P, P])
+        nc.tensor.transpose(factor_bank[:], factor_rows[:], ident[:])
+        factor_cols = sb("factor_cols", [P, 2 * PACK], F32)
+        nc.scalar.copy(out=factor_cols[:], in_=factor_bank[:, 0:2 * PACK])
         si_bank = new_bank([P, K])
-        for r in range(PACK):
-            nc.tensor.transpose(si_bank[:, r * P:(r + 1) * P], si_col[:, r:r + 1].to_broadcast([P, P]), ident[:])
+        for a in range(PACK):
+            nc.tensor.transpose(si_bank[:, a * P:(a + 1) * P], factor_cols[:, a:a + 1].to_broadcast([P, P]), ident[:])
+
         wT = sb("wT", [P, PACK * K], F32)
-        wT_view = wT[:].rearrange("p (n j r) -> p n j r", j=PACK, r=PACK)
-        for j in range(PACK):
-            w = sb("w%d" % j, [P, K], F32)
+
+        def turn_weights(c):
+            w = sb("w%d" % c, [P, K], F32)
             nc.vector.scalar_tensor_tensor(out=w[:].rearrange("p (r m) -> p m r", r=PACK),
-                                           in0=dz_raw[j].rearrange("p (m r) -> p m r", r=PACK),
-                                           scalar=cf_col[:, j:j + 1],
-                                           in1=si_bank[:].rearrange("p (r m) -> p m r", r=PACK),
-                                           op0=MULT, op1=MULT)
+                                           in0=dz_raw[c][:].rearrange("p (m r) -> p m r", r=PACK),
+                                           scalar=factor_cols[:, PACK + c:PACK + c + 1],
+                                           in1=si_bank[:].rearrange("p (m r) -> p m r", r=PACK),
+                                           op0=ALU.mult, op1=ALU.mult)
             bank = new_bank([P, PACK, P])
             for r in range(PACK):
                 nc.tensor.transpose(bank[:, r, :], w[:, r * P:(r + 1) * P], ident[:])
-            nc.scalar.copy(out=wT_view[:, :, j, :], in_=bank[:].rearrange("p r n -> p n r"))
+            nc.scalar.copy(out=chunks(wT, c).rearrange("p (n r) -> p n r", r=PACK), in_=bank[:].rearrange("p r n -> p n r"))
+
+        for c in range(PACK):
+            turn_weights(c)
 
         x_d = sb("x_d", [P, PACK * K], BF16)
-        x_d_view = x_d[:].rearrange("p (r m t) -> p m t r", r=PACK, t=PACK)
-        for a in range(2):
-            nc.vector.tensor_copy(out=x_d_view[:, a * 64:(a + 1) * 64, :, :],
-                                  in_=x_raw[a][:].rearrange("p t (m r) -> p m t r", r=PACK))
-        xd_mx = mx_tiles("xd")
-        quantize(xd_mx, E4M3, x_d[:], 0, 4)
-
-        x_i = sb("x_i", [P, PACK * K], BF16)
-        x_banks = [turn_pair(x_d, h) for h in range(2)]
+        nc.vector.tensor_copy(out=x_d[:].rearrange("p (r m t) -> p m t r", r=PACK, t=PACK),
+                              in_=x_raw[:].rearrange("p t (m r) -> p m t r", r=PACK))
+        xd_mx = mx_tiles("xd", K)
+        quantize(xd_mx, E4M3, x_d[:], 0)
 
         u_b = sb("u_b", [P, PACK * K], BF16)
-        u_mx = mx_tiles("u")
-        dv_b = sb("dv_b", [P, PACK * K], BF16, "u_raw1")
-        dv_mx = mx_tiles("dv")
-        for c in range(2):
-            cast_weights(chunks(u_b, c), u_raw, c, 1, nc.scalar.copy)
-        cast_weights(chunks(u_b, 2, 2), u_raw, 2, 2, nc.vector.tensor_copy)
-        for c in range(2):
-            quantize(u_mx, E4M3, chunks(u_b, c), c)
-        quantize(u_mx, E4M3, chunks(u_b, 2, 2), 2, 2)
-        for h in range(2):
-            unturn_pair(x_banks[h], x_i, h)
+        u_mx = mx_tiles("u", K)
         for c in range(PACK):
-            weigh(c, project(c, xd_mx, u_mx), wT, dv_b)
-        quantize(dv_mx, E5M2, dv_b[:], 0, 4)
+            copy = nc.vector.tensor_copy if c < 2 else nc.scalar.copy
+            cast_weights(chunks(u_b, c), u_raw[:, :, c * P:(c + 1) * P], copy)
+            quantize(u_mx, E4M3, chunks(u_b, c), c)
+        dv_b = [sb("dv_b%d" % h, [P, 2 * K], BF16) for h in range(2)]
+        for c in range(PACK):
+            weigh(project(c, xd_mx, u_mx), c, chunks(dv_b[c // 2], c % 2))
 
-        g_e = sb("g_e", [P, PACK * K], BF16)
-        g_e_view = g_e[:].rearrange("p (r m t) -> p m t r", r=PACK, t=PACK)
+        x_i = sb("x_i", [P, PACK * K], BF16)
+        x_words = x_d[:].bitcast(F32)
+        for h in range(2):
+            bank = new_bank([P, PACK, P])
+            for r in range(PACK):
+                nc.tensor.transpose(bank[:, r, :], x_words[:, 2 * P * r + h:2 * P * (r + 1):2], ident[:])
+            halves = bank[:].rearrange("p r n -> p (r n)").bitcast(BF16)
+            nc.scalar.copy(out=chunks(x_i, 2 * h, 2).rearrange("p (e n r) -> p e n r", e=2, r=PACK),
+                           in_=halves.rearrange("p (r n e) -> p e n r", r=PACK, e=2))
+
         planes = [sb("planes%d" % h, [P, 2 * K], BF16) for h in range(2)]
-
-        def weave(h, copy):
-            copy(out=g_e_view[:, :, 2 * h:2 * h + 2, :],
-                 in_=planes[h][:].rearrange("p (t m r) -> p m t r", t=2, r=PACK))
-
         for t in range(PACK):
             nc.vector.tensor_copy(chunks(planes[t // 2], t % 2), table[t][:].indirect(offsets[:]))
-            if t % 2 == 1:
-                weave(t // 2, nc.vector.tensor_copy)
-        g_i0 = sb("g_i0", [P, 2 * K], BF16)
-        turn_planes(planes[0], g_i0)
-        gi_mx = [mx_tiles("gi0", 2 * P, "table2"), mx_tiles("gi1", 2 * P)]
-        quantize(gi_mx[0], E4M3, g_i0[:], 0, 2)
-        early = [gradient_mm(gi_mx[0], t, dv_mx) for t in range(2)]
+        d_mx = mx_tiles("d", 2 * K, "table1")
+        for h in range(2):
+            quantize(d_mx, E5M2, dv_b[h][:], 2 * h)
+        g_i = [sb("g_i%d" % t, [P, K], BF16) for t in range(2)]
+        for t in range(2):
+            turn_planes(chunks(planes[0], t), g_i[t][:])
+        g_e = sb("g_e", [P, PACK * K], BF16, "dv_b1")
+        g_e_view = g_e[:].rearrange("p (r m t) -> p m t r", r=PACK, t=PACK)
+        for h, copy in enumerate([nc.scalar.copy, nc.vector.tensor_copy]):
+            copy(out=g_e_view[:, :, 2 * h:2 * h + 2, :],
+                 in_=planes[h][:].rearrange("p (t m r) -> p m t r", t=2, r=PACK))
+        gi0_mx = mx_tiles("gi0", P, "dv_b0")
+        quantize(gi0_mx, E4M3, g_i[0][:], 0)
+        store_out_1(0, gi0_mx, 0)
+        xi_mx = mx_tiles("xi", K + P, "table2")
+        quantize(xi_mx, E4M3, g_i[1][:], PACK)
+        store_out_1(1, xi_mx, PACK)
+        quantize(xi_mx, E4M3, x_i[:], 0)
 
-        v_b = [sb("v_b%d" % c, [P, K], BF16) for c in range(PACK)]
-        for c in range(PACK):
-            cast_weights(v_b[c][:], v_raw, c, 1, nc.scalar.copy)
-        v_mx = mx_tiles("v")
-        quantize(v_mx, E4M3, v_b[0][:], 0)
+        v_mx = mx_tiles("v", K)
+
+        def quantize_v(c, v_b):
+            cast_weights(v_b, v_raw[c // 2][:, :, (c % 2) * P:(c % 2 + 1) * P], nc.scalar.copy)
+            quantize(v_mx, E4M3, v_b, c)
+
+        quantize_v(0, sb("v_b0", [P, K], BF16)[:])
         ge_mx = mx_tiles("ge", K, "v_b0")
-        du_b = sb("du_b", [P, PACK * K], BF16)
-        du_mx = mx_tiles("du")
         for r in range(PACK):
             quantize(ge_mx, E4M3, chunks(g_e, r), r)
-        g_i1 = sb("g_i1", [P, 2 * K], BF16, tag="v_raw0")
-        turn_planes(planes[1], g_i1)
-        banks = []
-        for c in range(PACK):
-            if c > 0:
-                quantize(v_mx, E4M3, v_b[c][:], c)
-            banks.append(project(c, ge_mx, v_mx))
-        xi_mx = mx_tiles("xi", K, "g_e")
-        quantize(xi_mx, E4M3, x_i[:], 0, 4)
-        quantize(gi_mx[1], E4M3, g_i1[:], 0, 2)
-        res1 = sb("res1", [P, 2, K], F32, "v_raw1")
-        for t in range(2):
-            store(early[t], res1[:, t, :], out_1, t, nc.scalar.copy)
+        quantize_v(1, sb("v_b1", [P, K], BF16)[:])
+        late = sb("late", [P, PACK * K], BF16, "v_raw0")
+        turn_planes(planes[1][:], chunks(late, 0, 2))
+        v_banks = [project(c, ge_mx, v_mx) for c in range(2)]
+        late_mx = mx_tiles("late", 2 * P)
+        quantize(late_mx, E4M3, chunks(late, 0, 2), 0)
+        for c in range(2, PACK):
+            quantize_v(c, chunks(late, c))
         for t in range(2, PACK):
-            res = sb("res1_%d" % t, [P, K], F32)
-            store(gradient_mm(gi_mx[1], t - 2, dv_mx), res[:], out_1, t, nc.scalar.copy)
+            store_out_1(t, late_mx, t - 2)
+        v_banks.extend([project(c, ge_mx, v_mx) for c in range(2, PACK)])
+
+        du_b = sb("du_b", [P, PACK * K], BF16)
         for c in range(PACK):
-            weigh(c, banks[c], wT, du_b)
+            weigh(v_banks[c], c, chunks(du_b, c))
             if c > 0:
-                quantize(du_mx, E5M2, chunks(du_b, c - 1), c - 1)
-        quantize(du_mx, E5M2, chunks(du_b, PACK - 1), PACK - 1)
-        for t in range(PACK):
-            res = sb("res0_%d" % t, [P, K], F32)
-            store(gradient_mm(xi_mx, t, du_mx), res[:], out_0, t, nc.vector.tensor_copy if t % 2 == 0 else nc.scalar.copy)
+                quantize(d_mx, E5M2, chunks(du_b, c - 1), PACK + c - 1)
+        quantize(d_mx, E5M2, chunks(du_b, PACK - 1), 2 * PACK - 1)
+        for half, copies in enumerate([[nc.scalar.copy, nc.scalar.copy], [nc.vector.tensor_copy, nc.scalar.copy]]):
+            for t in range(PACK):
+                res = sb("res0_%d_%d" % (half, t), [P, HALF], F32)
+                copies[t % 2](out=res[:], in_=gradient(xi_mx, t, (half + 1) * HALF)[:, HALF:K])
+                nc.sync.dma_start(out=by_place(out_0)[:, t, half * HALF:(half + 1) * HALF], in_=res[:])

@@ -43,13 +43,11 @@ def tile_attend_gbpool_UV_kernel(tc, xT, dz, cf, si, U, eT, V, offs, out_0, out_
             nc.sync.dma_start(out=tile[:], in_=src)
             return tile
 
-        factor_rows = sb("factor_rows", [P, P], F32)
-        nc.vector.memset(factor_rows[:], 0.0)
-        nc.scalar.dma_start(out=factor_rows[0:PACK, :], in_=si[0:1, :].rearrange("o (a m) -> (o a) m", a=PACK))
-        nc.scalar.dma_start(out=factor_rows[PACK:2 * PACK, :], in_=cf.rearrange("(c n) o -> c (n o)", c=PACK))
-        dz_raw = [load("dz_raw%d" % c, dz[c * P:(c + 1) * P, :]) for c in range(PACK)]
-        x_raw = load("x_raw", by_place(xT))
-        u_raw = load("u_raw", by_place(U))
+        si_col = load("si_col", si[0:1, :].rearrange("o (m r) -> m (o r)", r=PACK))
+        cf_col = load("cf_col", cf.rearrange("(p j) o -> p (j o)", j=PACK))
+        dz_raw = [load("dz_raw%d" % h, by_place(dz)[:, 2 * h:2 * h + 2, :]) for h in range(2)]
+        x_raw = [load("x_raw%d" % h, by_place(xT)[:, 2 * h:2 * h + 2, :]) for h in range(2)]
+        u_raw = [load("u_raw%d" % a, by_place(U)[:, :, a * HALF:(a + 1) * HALF]) for a in range(2)]
         offsets = keep.tile([P, K // 16], U16, name="offsets")
         nc.sync.dma_start(offsets[:], offs)
         table = [load("table%d" % t, by_place(eT)[:, t, :]) for t in range(PACK)]
@@ -114,42 +112,36 @@ def tile_attend_gbpool_UV_kernel(tc, xT, dz, cf, si, U, eT, V, offs, out_0, out_
             nc.scalar.copy(out=res[:], in_=gradient(act_mx, c, 0)[:])
             nc.sync.dma_start(out=by_place(out_1)[:, t, :], in_=res[:])
 
-        factor_bank = new_bank([P, P])
-        nc.tensor.transpose(factor_bank[:], factor_rows[:], ident[:])
-        factor_cols = sb("factor_cols", [P, 2 * PACK], F32)
-        nc.scalar.copy(out=factor_cols[:], in_=factor_bank[:, 0:2 * PACK])
-        si_bank = new_bank([P, K])
-        for a in range(PACK):
-            nc.tensor.transpose(si_bank[:, a * P:(a + 1) * P], factor_cols[:, a:a + 1].to_broadcast([P, P]), ident[:])
-
+        si_bank = new_bank([P, PACK, P])
+        for r in range(PACK):
+            nc.tensor.transpose(si_bank[:, r, :], si_col[:, r:r + 1].to_broadcast([P, P]), ident[:])
         wT = sb("wT", [P, PACK * K], F32)
-
-        def turn_weights(c):
-            w = sb("w%d" % c, [P, K], F32)
+        wT_view = wT[:].rearrange("p (n j r) -> p n j r", j=PACK, r=PACK)
+        for j in range(PACK):
+            w = sb("w%d" % j, [P, K], F32)
             nc.vector.scalar_tensor_tensor(out=w[:].rearrange("p (r m) -> p m r", r=PACK),
-                                           in0=dz_raw[c][:].rearrange("p (m r) -> p m r", r=PACK),
-                                           scalar=factor_cols[:, PACK + c:PACK + c + 1],
-                                           in1=si_bank[:].rearrange("p (m r) -> p m r", r=PACK),
+                                           in0=dz_raw[j // 2][:, j % 2, :].rearrange("p (m r) -> p m r", r=PACK),
+                                           scalar=cf_col[:, j:j + 1],
+                                           in1=si_bank[:].rearrange("p r m -> p m r"),
                                            op0=ALU.mult, op1=ALU.mult)
             bank = new_bank([P, PACK, P])
             for r in range(PACK):
                 nc.tensor.transpose(bank[:, r, :], w[:, r * P:(r + 1) * P], ident[:])
-            nc.scalar.copy(out=chunks(wT, c).rearrange("p (n r) -> p n r", r=PACK), in_=bank[:].rearrange("p r n -> p n r"))
-
-        for c in range(PACK):
-            turn_weights(c)
+            nc.scalar.copy(out=wT_view[:, :, j, :], in_=bank[:].rearrange("p r n -> p n r"))
 
         x_d = sb("x_d", [P, PACK * K], BF16)
-        nc.vector.tensor_copy(out=x_d[:].rearrange("p (r m t) -> p m t r", r=PACK, t=PACK),
-                              in_=x_raw[:].rearrange("p t (m r) -> p m t r", r=PACK))
+        x_d_view = x_d[:].rearrange("p (r m t) -> p m r t", r=PACK, t=PACK)
+        for h in range(2):
+            nc.vector.tensor_copy(out=x_d_view[:, :, :, 2 * h:2 * h + 2],
+                                  in_=x_raw[h][:].rearrange("p t (m r) -> p m r t", r=PACK))
         xd_mx = mx_tiles("xd", K)
         quantize(xd_mx, E4M3, x_d[:], 0)
 
         u_b = sb("u_b", [P, PACK * K], BF16)
         u_mx = mx_tiles("u", K)
         for c in range(PACK):
-            copy = nc.vector.tensor_copy if c < 2 else nc.scalar.copy
-            cast_weights(chunks(u_b, c), u_raw[:, :, c * P:(c + 1) * P], copy)
+            copy = nc.scalar.copy if c != 2 else nc.vector.tensor_copy
+            cast_weights(chunks(u_b, c), u_raw[c // 2][:, :, (c % 2) * P:(c % 2 + 1) * P], copy)
             quantize(u_mx, E4M3, chunks(u_b, c), c)
         dv_b = [sb("dv_b%d" % h, [P, 2 * K], BF16) for h in range(2)]
         for c in range(PACK):
@@ -166,8 +158,11 @@ def tile_attend_gbpool_UV_kernel(tc, xT, dz, cf, si, U, eT, V, offs, out_0, out_
                            in_=halves.rearrange("p (r n e) -> p e n r", r=PACK, e=2))
 
         planes = [sb("planes%d" % h, [P, 2 * K], BF16) for h in range(2)]
-        for t in range(PACK):
+        for t in range(PACK - 1):
             nc.vector.tensor_copy(chunks(planes[t // 2], t % 2), table[t][:].indirect(offsets[:]))
+        for a in range(2):
+            nc.vector.tensor_copy(chunks(planes[1], 1)[:, a * HALF:(a + 1) * HALF],
+                                  table[PACK - 1][:].indirect(offsets[:, a * HALF // 16:(a + 1) * HALF // 16]))
         d_mx = mx_tiles("d", 2 * K, "table1")
         for h in range(2):
             quantize(d_mx, E5M2, dv_b[h][:], 2 * h)
@@ -175,10 +170,11 @@ def tile_attend_gbpool_UV_kernel(tc, xT, dz, cf, si, U, eT, V, offs, out_0, out_
         for t in range(2):
             turn_planes(chunks(planes[0], t), g_i[t][:])
         g_e = sb("g_e", [P, PACK * K], BF16, "dv_b1")
-        g_e_view = g_e[:].rearrange("p (r m t) -> p m t r", r=PACK, t=PACK)
-        for h, copy in enumerate([nc.scalar.copy, nc.vector.tensor_copy]):
-            copy(out=g_e_view[:, :, 2 * h:2 * h + 2, :],
-                 in_=planes[h][:].rearrange("p (t m r) -> p m t r", t=2, r=PACK))
+        g_e_view = g_e[:].rearrange("p (r m t) -> p m r t", r=PACK, t=PACK)
+        pairs = [planes[h][:].rearrange("p (t m r) -> p m r t", t=2, r=PACK) for h in range(2)]
+        nc.scalar.copy(out=g_e_view[:, :, :, 0:2], in_=pairs[0])
+        for a in range(2):
+            nc.vector.tensor_copy(out=g_e_view[:, a * P // 2:(a + 1) * P // 2, :, 2:4], in_=pairs[1][:, a * P // 2:(a + 1) * P // 2])
         gi0_mx = mx_tiles("gi0", P, "dv_b0")
         quantize(gi0_mx, E4M3, g_i[0][:], 0)
         store_out_1(0, gi0_mx, 0)
@@ -205,9 +201,10 @@ def tile_attend_gbpool_UV_kernel(tc, xT, dz, cf, si, U, eT, V, offs, out_0, out_
         quantize(late_mx, E4M3, chunks(late, 0, 2), 0)
         for c in range(2, PACK):
             quantize_v(c, chunks(late, c))
-        for t in range(2, PACK):
-            store_out_1(t, late_mx, t - 2)
-        v_banks.extend([project(c, ge_mx, v_mx) for c in range(2, PACK)])
+        store_out_1(2, late_mx, 0)
+        v_banks.append(project(2, ge_mx, v_mx))
+        store_out_1(3, late_mx, 1)
+        v_banks.append(project(3, ge_mx, v_mx))
 
         du_b = sb("du_b", [P, PACK * K], BF16)
         for c in range(PACK):

@@ -119,14 +119,14 @@ def tile_attend_gbpool_UV_kernel(tc, xT, dz, cf, si, U, eT, V, offs, out_0, out_
         wT_view = wT[:].rearrange("p (n j r) -> p n j r", j=PACK, r=PACK)
         for j in range(PACK):
             w = sb("w%d" % j, [P, K], F32)
-            nc.vector.scalar_tensor_tensor(out=w[:].rearrange("p (r m) -> p m r", r=PACK),
+            nc.vector.scalar_tensor_tensor(out=w[:].rearrange("p (m r) -> p m r", r=PACK),
                                            in0=dz_raw[j // 2][:, j % 2, :].rearrange("p (m r) -> p m r", r=PACK),
                                            scalar=cf_col[:, j:j + 1],
                                            in1=si_bank[:].rearrange("p r m -> p m r"),
                                            op0=ALU.mult, op1=ALU.mult)
             bank = new_bank([P, PACK, P])
             for r in range(PACK):
-                nc.tensor.transpose(bank[:, r, :], w[:, r * P:(r + 1) * P], ident[:])
+                nc.tensor.transpose(bank[:, r, :], w[:, r:K:PACK], ident[:])
             nc.scalar.copy(out=wT_view[:, :, j, :], in_=bank[:].rearrange("p r n -> p n r"))
 
         x_d = sb("x_d", [P, PACK * K], BF16)
@@ -140,10 +140,10 @@ def tile_attend_gbpool_UV_kernel(tc, xT, dz, cf, si, U, eT, V, offs, out_0, out_
         u_b = sb("u_b", [P, PACK * K], BF16)
         u_mx = mx_tiles("u", K)
         for c in range(PACK):
-            copy = nc.scalar.copy if c != 2 else nc.vector.tensor_copy
+            copy = nc.scalar.copy if c == PACK - 1 else nc.vector.tensor_copy
             cast_weights(chunks(u_b, c), u_raw[c // 2][:, :, (c % 2) * P:(c % 2 + 1) * P], copy)
             quantize(u_mx, E4M3, chunks(u_b, c), c)
-        dv_b = [sb("dv_b%d" % h, [P, 2 * K], BF16) for h in range(2)]
+        dv_b = [sb("dv_b0", [P, 2 * K], BF16, "u_raw1"), sb("dv_b1", [P, 2 * K], BF16)]
         for c in range(PACK):
             weigh(project(c, xd_mx, u_mx), c, chunks(dv_b[c // 2], c % 2))
 
@@ -172,10 +172,10 @@ def tile_attend_gbpool_UV_kernel(tc, xT, dz, cf, si, U, eT, V, offs, out_0, out_
         g_e = sb("g_e", [P, PACK * K], BF16, "dv_b1")
         g_e_view = g_e[:].rearrange("p (r m t) -> p m r t", r=PACK, t=PACK)
         pairs = [planes[h][:].rearrange("p (t m r) -> p m r t", t=2, r=PACK) for h in range(2)]
-        nc.scalar.copy(out=g_e_view[:, :, :, 0:2], in_=pairs[0])
+        nc.scalar.copy(out=g_e_view[:, :, :, 0:2].rearrange("p m r t -> p r m t"), in_=pairs[0].rearrange("p m r t -> p r m t"))
         for a in range(2):
             nc.vector.tensor_copy(out=g_e_view[:, a * P // 2:(a + 1) * P // 2, :, 2:4], in_=pairs[1][:, a * P // 2:(a + 1) * P // 2])
-        gi0_mx = mx_tiles("gi0", P, "dv_b0")
+        gi0_mx = mx_tiles("gi0", P, "u_raw1")
         quantize(gi0_mx, E4M3, g_i[0][:], 0)
         store_out_1(0, gi0_mx, 0)
         xi_mx = mx_tiles("xi", K + P, "table2")

@@ -10,6 +10,7 @@ U8 = mybir.dt.uint8
 E4M3 = mybir.dt.float8_e4m3fn_x4
 E5M2 = mybir.dt.float8_e5m2_x4
 ALU = mybir.AluOpType
+COPY = mybir.ActivationFunctionType.Copy
 
 P = 128
 PACK = 4
@@ -38,20 +39,21 @@ def tile_attend_gbpool_UV_kernel(tc, xT, dz, cf, si, U, eT, V, offs, out_0, out_
         def by_place(dram):
             return dram.rearrange("(p t) c -> p t c", t=PACK)
 
-        def load(name, src):
+        def load(name, src, queue=nc.sync):
             tile = sb(name, src.shape, F32)
-            nc.sync.dma_start(out=tile[:], in_=src)
+            queue.dma_start(out=tile[:], in_=src)
             return tile
 
-        si_col = load("si_col", si[0:1, :].rearrange("o (m r) -> m (o r)", r=PACK))
-        cf_col = load("cf_col", cf.rearrange("(p j) o -> p (j o)", j=PACK))
-        dz_raw = [load("dz_raw%d" % h, by_place(dz)[:, 2 * h:2 * h + 2, :]) for h in range(2)]
         x_raw = [load("x_raw%d" % h, by_place(xT)[:, 2 * h:2 * h + 2, :]) for h in range(2)]
+        si_col = load("si_col", si[0:1, :].rearrange("o (m r) -> m (o r)", r=PACK), nc.scalar)
+        cf_col = load("cf_col", cf.rearrange("(p j) o -> p (j o)", j=PACK), nc.scalar)
+        dz_raw = [load("dz_raw%d" % h, by_place(dz)[:, 2 * h:2 * h + 2, :]) for h in range(2)]
         u_raw = [load("u_raw%d" % a, by_place(U)[:, :, a * HALF:(a + 1) * HALF]) for a in range(2)]
+        table = [load("table0", by_place(eT)[:, 0, :])]
         offsets = keep.tile([P, K // 16], U16, name="offsets")
         nc.sync.dma_start(offsets[:], offs)
-        table = [load("table%d" % t, by_place(eT)[:, t, :]) for t in range(PACK)]
-        v_raw = [load("v_raw%d" % a, by_place(V)[:, :, a * HALF:(a + 1) * HALF]) for a in range(2)]
+        table.extend([load("table%d" % t, by_place(eT)[:, t, :]) for t in range(1, PACK)])
+        v_raw = [load("v_raw%d" % c, by_place(V)[:, :, c * P:(c + 1) * P]) for c in range(PACK)]
 
         ones = sb("ones", [P, P], F32)
         nc.vector.memset(ones[:], 1.0)
@@ -89,15 +91,18 @@ def tile_attend_gbpool_UV_kernel(tc, xT, dz, cf, si, U, eT, V, offs, out_0, out_
             nc.vector.tensor_tensor(out=dst.rearrange("p (n r) -> p n r", r=PACK), in0=bank[:].rearrange("p r n -> p n r"),
                                     in1=chunks(wT, c).rearrange("p (n r) -> p n r", r=PACK), op=ALU.mult)
 
-        def turn_planes(src, dst):
+        def turn_planes(src):
             n = src.shape[1] // K
             words = src.bitcast(F32)
             bank = new_bank([P, 2 * n, P])
             for e in range(n):
                 for u in range(2):
                     nc.tensor.transpose(bank[:, 2 * e + u, :], words[:, 2 * P * e + u:2 * P * (e + 1):2], ident[:])
-            nc.scalar.copy(out=dst.bitcast(F32).rearrange("p (e n u) -> p e n u", e=n, u=2),
-                           in_=bank[:].rearrange("p (e u) n -> p e n u", u=2))
+            return bank
+
+        def weave_turned(bank, dst, copy):
+            copy(out=dst.bitcast(F32).rearrange("p (e n u) -> p e n u", n=P, u=2),
+                 in_=bank[:].rearrange("p (e u) n -> p e n u", u=2))
 
         def gradient(act_mx, c, first):
             bank = new_bank([P, K])
@@ -107,27 +112,18 @@ def tile_attend_gbpool_UV_kernel(tc, xT, dz, cf, si, U, eT, V, offs, out_0, out_
                                 rhs=d_mx[0][:, window].bitcast(E5M2), rhs_scale=d_mx[1][:, window], start=True, stop=True)
             return bank
 
-        def store_out_1(t, act_mx, c):
-            res = sb("res1_%d" % t, [P, K], F32)
-            nc.scalar.copy(out=res[:], in_=gradient(act_mx, c, 0)[:])
-            nc.sync.dma_start(out=by_place(out_1)[:, t, :], in_=res[:])
+        def store_out_1(t, banks, slot=None):
+            res = sb("res1_%d" % t, [P, len(banks), K], F32, slot)
+            for e, bank in enumerate(banks):
+                nc.scalar.copy(out=res[:, e, :], in_=bank[:])
+                nc.sync.dma_start(out=by_place(out_1)[:, t + e, :], in_=res[:, e, :])
 
-        si_bank = new_bank([P, PACK, P])
-        for r in range(PACK):
-            nc.tensor.transpose(si_bank[:, r, :], si_col[:, r:r + 1].to_broadcast([P, P]), ident[:])
-        wT = sb("wT", [P, PACK * K], F32)
-        wT_view = wT[:].rearrange("p (n j r) -> p n j r", j=PACK, r=PACK)
-        for j in range(PACK):
-            w = sb("w%d" % j, [P, K], F32)
-            nc.vector.scalar_tensor_tensor(out=w[:].rearrange("p (m r) -> p m r", r=PACK),
-                                           in0=dz_raw[j // 2][:, j % 2, :].rearrange("p (m r) -> p m r", r=PACK),
-                                           scalar=cf_col[:, j:j + 1],
-                                           in1=si_bank[:].rearrange("p r m -> p m r"),
-                                           op0=ALU.mult, op1=ALU.mult)
-            bank = new_bank([P, PACK, P])
-            for r in range(PACK):
-                nc.tensor.transpose(bank[:, r, :], w[:, r:K:PACK], ident[:])
-            nc.scalar.copy(out=wT_view[:, :, j, :], in_=bank[:].rearrange("p r n -> p n r"))
+        def store_out_0(half, copies, rows):
+            for t in range(0, PACK, rows):
+                res = sb("res0_%d_%d" % (half, t), [P, rows, HALF], F32)
+                for e in range(rows):
+                    copies[(t + e) % 2](out=res[:, e, :], in_=gradient(xi_mx, t + e, (half + 1) * HALF)[:, HALF:K])
+                nc.sync.dma_start(out=by_place(out_0)[:, t:t + rows, half * HALF:(half + 1) * HALF], in_=res[:])
 
         x_d = sb("x_d", [P, PACK * K], BF16)
         x_d_view = x_d[:].rearrange("p (r m t) -> p m r t", r=PACK, t=PACK)
@@ -136,20 +132,10 @@ def tile_attend_gbpool_UV_kernel(tc, xT, dz, cf, si, U, eT, V, offs, out_0, out_
                                   in_=x_raw[h][:].rearrange("p t (m r) -> p m r t", r=PACK))
         xd_mx = mx_tiles("xd", K)
         quantize(xd_mx, E4M3, x_d[:], 0)
-
-        u_b = sb("u_b", [P, PACK * K], BF16)
-        u_mx = mx_tiles("u", K)
-        for c in range(PACK):
-            copy = nc.scalar.copy if c == PACK - 1 else nc.vector.tensor_copy
-            cast_weights(chunks(u_b, c), u_raw[c // 2][:, :, (c % 2) * P:(c % 2 + 1) * P], copy)
-            quantize(u_mx, E4M3, chunks(u_b, c), c)
-        dv_b = [sb("dv_b0", [P, 2 * K], BF16, "u_raw1"), sb("dv_b1", [P, 2 * K], BF16)]
-        for c in range(PACK):
-            weigh(project(c, xd_mx, u_mx), c, chunks(dv_b[c // 2], c % 2))
-
         x_i = sb("x_i", [P, PACK * K], BF16)
         x_words = x_d[:].bitcast(F32)
-        for h in range(2):
+
+        def turn_x(h):
             bank = new_bank([P, PACK, P])
             for r in range(PACK):
                 nc.tensor.transpose(bank[:, r, :], x_words[:, 2 * P * r + h:2 * P * (r + 1):2], ident[:])
@@ -157,63 +143,125 @@ def tile_attend_gbpool_UV_kernel(tc, xT, dz, cf, si, U, eT, V, offs, out_0, out_
             nc.scalar.copy(out=chunks(x_i, 2 * h, 2).rearrange("p (e n r) -> p e n r", e=2, r=PACK),
                            in_=halves.rearrange("p (r n e) -> p e n r", r=PACK, e=2))
 
-        planes = [sb("planes%d" % h, [P, 2 * K], BF16) for h in range(2)]
-        for t in range(PACK - 1):
-            nc.vector.tensor_copy(chunks(planes[t // 2], t % 2), table[t][:].indirect(offsets[:]))
-        for a in range(2):
-            nc.vector.tensor_copy(chunks(planes[1], 1)[:, a * HALF:(a + 1) * HALF],
-                                  table[PACK - 1][:].indirect(offsets[:, a * HALF // 16:(a + 1) * HALF // 16]))
-        d_mx = mx_tiles("d", 2 * K, "table1")
+        turn_x(0)
+        si_bank = new_bank([P, PACK, P])
+        for r in range(PACK):
+            nc.tensor.transpose(si_bank[:, r, :], si_col[:, r:r + 1].to_broadcast([P, P]), ident[:])
+        turn_x(1)
+
+        wT = sb("wT", [P, PACK * K], F32)
+        wT_view = wT[:].rearrange("p (n j r) -> p n j r", j=PACK, r=PACK)
+        for j in range(PACK):
+            w = sb("w%d" % j, [P, K], F32)
+            nc.vector.scalar_tensor_tensor(out=w[:].rearrange("p (r m) -> p m r", r=PACK),
+                                           in0=dz_raw[j // 2][:, j % 2, :].rearrange("p (m r) -> p m r", r=PACK),
+                                           scalar=cf_col[:, j:j + 1],
+                                           in1=si_bank[:].rearrange("p r m -> p m r"),
+                                           op0=ALU.mult, op1=ALU.mult)
+            bank = new_bank([P, PACK, P])
+            for r in range(PACK):
+                nc.tensor.transpose(bank[:, r, :], w[:, r * P:(r + 1) * P], ident[:])
+            nc.scalar.copy(out=wT_view[:, :, j, :], in_=bank[:].rearrange("p r n -> p n r"))
+
+        u_b = sb("u_b", [P, PACK * K], BF16)
+        u_mx = mx_tiles("u", K)
+        dv_b = sb("dv_b", [P, PACK * K], BF16)
+
+        def cast_u(c, copy):
+            cast_weights(chunks(u_b, c), u_raw[c // 2][:, :, (c % 2) * P:(c % 2 + 1) * P], copy)
+
+        def u_panel(c):
+            quantize(u_mx, E4M3, chunks(u_b, c), c)
+            return project(c, xd_mx, u_mx)
+
+        for c in range(2):
+            cast_u(c, nc.vector.tensor_copy)
+        u_banks = [u_panel(c) for c in range(2)]
+        xi_mx = mx_tiles("xi", K, "dz_raw1")
+        quantize(xi_mx, E4M3, x_i[:], 0)
+        cast_u(2, nc.vector.tensor_copy)
+        cast_u(3, nc.scalar.copy)
+        for c in range(PACK):
+            weigh(u_banks[c], c, chunks(dv_b, c))
+            if c < 2:
+                u_banks.append(u_panel(c + 2))
+        d_mx = mx_tiles("d", 2 * K)
         for h in range(2):
-            quantize(d_mx, E5M2, dv_b[h][:], 2 * h)
-        g_i = [sb("g_i%d" % t, [P, K], BF16) for t in range(2)]
-        for t in range(2):
-            turn_planes(chunks(planes[0], t), g_i[t][:])
-        g_e = sb("g_e", [P, PACK * K], BF16, "dv_b1")
+            quantize(d_mx, E5M2, chunks(dv_b, 2 * h, 2), 2 * h)
+
+        planes = [sb("planes%d" % h, [P, 2 * K], BF16) for h in range(2)]
+        g_e = sb("g_e", [P, PACK * K], BF16)
         g_e_view = g_e[:].rearrange("p (r m t) -> p m r t", r=PACK, t=PACK)
         pairs = [planes[h][:].rearrange("p (t m r) -> p m r t", t=2, r=PACK) for h in range(2)]
-        nc.scalar.copy(out=g_e_view[:, :, :, 0:2].rearrange("p m r t -> p r m t"), in_=pairs[0].rearrange("p m r t -> p r m t"))
+
+        def gather(t, first, count):
+            nc.vector.tensor_copy(chunks(planes[t // 2], t % 2)[:, first:first + count],
+                                  table[t][:].indirect(offsets[:, first // 16:(first + count) // 16]))
+
+        def turn(t):
+            g_i = sb("g_i%d" % t, [P, K], BF16)
+            weave_turned(turn_planes(chunks(planes[t // 2], t % 2)), g_i[:], nc.scalar.copy)
+            return g_i
+
+        def quantize_turned(t, g_i, slot=None):
+            gi_mx = mx_tiles("gi%d" % t, P, slot)
+            quantize(gi_mx, E4M3, g_i[:], 0)
+            return gi_mx
+
+        table0_b = sb("table0_b", [P, ITEMS], BF16)
+        nc.scalar.activation(out=table0_b[:], in_=table[0][:], func=COPY)
+        nc.scalar.activation(out=chunks(planes[0], 0), in_=table0_b[:].indirect(offsets[:]), func=COPY)
+        gather(1, 0, K)
+        g_i01 = sb("g_i01", [P, 2 * K], BF16)
+        for t in range(2):
+            weave_turned(turn_planes(chunks(planes[0], t)), chunks(g_i01, t), nc.scalar.copy)
+        for a in range(2):
+            nc.scalar.copy(out=g_e_view[:, :, 2 * a:2 * a + 2, 0:2].rearrange("p m r t -> p r m t"),
+                           in_=pairs[0][:, :, 2 * a:2 * a + 2, :].rearrange("p m r t -> p r m t"))
+        gather(2, 0, K)
+        gi01_mx = mx_tiles("gi01", 2 * P, "table2")
+        quantize(gi01_mx, E4M3, g_i01[:], 0)
+        g_i2 = turn(2)
+        out_1_banks = [gradient(gi01_mx, t, 0) for t in range(2)]
+        for a in range(2):
+            gather(3, a * HALF, HALF)
         for a in range(2):
             nc.vector.tensor_copy(out=g_e_view[:, a * P // 2:(a + 1) * P // 2, :, 2:4], in_=pairs[1][:, a * P // 2:(a + 1) * P // 2])
-        gi0_mx = mx_tiles("gi0", P, "u_raw1")
-        quantize(gi0_mx, E4M3, g_i[0][:], 0)
-        store_out_1(0, gi0_mx, 0)
-        xi_mx = mx_tiles("xi", K + P, "table2")
-        quantize(xi_mx, E4M3, g_i[1][:], PACK)
-        store_out_1(1, xi_mx, PACK)
-        quantize(xi_mx, E4M3, x_i[:], 0)
+        g3_bank = turn_planes(chunks(planes[1], 1))
 
+        v_b = [sb("v_b%d" % c, [P, K], BF16)[:] for c in range(PACK)]
+        for c in range(PACK - 1):
+            cast_weights(v_b[c], v_raw[c][:], nc.scalar.copy)
+        g_i3 = sb("g_i3", [P, K], BF16, "v_raw1")
+        weave_turned(g3_bank, g_i3[:], nc.scalar.copy)
+        cast_weights(v_b[PACK - 1], v_raw[PACK - 1][:], nc.scalar.copy)
         v_mx = mx_tiles("v", K)
+        quantize(v_mx, E4M3, v_b[0], 0)
+        ge_mx = mx_tiles("ge", K, "v_raw0")
+        for r in range(0, PACK, 2):
+            quantize(ge_mx, E4M3, chunks(g_e, r, 2), r)
+        v_banks = [project(0, ge_mx, v_mx)]
 
-        def quantize_v(c, v_b):
-            cast_weights(v_b, v_raw[c // 2][:, :, (c % 2) * P:(c % 2 + 1) * P], nc.scalar.copy)
-            quantize(v_mx, E4M3, v_b, c)
+        def v_panel(c):
+            quantize(v_mx, E4M3, v_b[c], c)
+            return project(c, ge_mx, v_mx)
 
-        quantize_v(0, sb("v_b0", [P, K], BF16)[:])
-        ge_mx = mx_tiles("ge", K, "v_b0")
-        for r in range(PACK):
-            quantize(ge_mx, E4M3, chunks(g_e, r), r)
-        quantize_v(1, sb("v_b1", [P, K], BF16)[:])
-        late = sb("late", [P, PACK * K], BF16, "v_raw0")
-        turn_planes(planes[1][:], chunks(late, 0, 2))
-        v_banks = [project(c, ge_mx, v_mx) for c in range(2)]
-        late_mx = mx_tiles("late", 2 * P)
-        quantize(late_mx, E4M3, chunks(late, 0, 2), 0)
-        for c in range(2, PACK):
-            quantize_v(c, chunks(late, c))
-        store_out_1(2, late_mx, 0)
-        v_banks.append(project(2, ge_mx, v_mx))
-        store_out_1(3, late_mx, 1)
-        v_banks.append(project(3, ge_mx, v_mx))
-
+        v_banks.append(v_panel(1))
+        gi2_mx = quantize_turned(2, g_i2, "v_b0")
+        out_1_banks.append(gradient(gi2_mx, 0, 0))
+        v_banks.append(v_panel(2))
         du_b = sb("du_b", [P, PACK * K], BF16)
-        for c in range(PACK):
+        weigh(v_banks[0], 0, chunks(du_b, 0))
+        gi3_mx = quantize_turned(3, g_i3)
+        out_1_banks.append(gradient(gi3_mx, 0, 0))
+        weigh(v_banks[1], 1, chunks(du_b, 1))
+        store_out_1(0, out_1_banks, "v_raw3")
+        quantize(d_mx, E5M2, chunks(du_b, 0), PACK)
+        v_banks.append(v_panel(3))
+        quantize(d_mx, E5M2, chunks(du_b, 1), PACK + 1)
+        for c in range(2, PACK):
             weigh(v_banks[c], c, chunks(du_b, c))
-            if c > 0:
-                quantize(d_mx, E5M2, chunks(du_b, c - 1), PACK + c - 1)
-        quantize(d_mx, E5M2, chunks(du_b, PACK - 1), 2 * PACK - 1)
-        for half, copies in enumerate([[nc.scalar.copy, nc.scalar.copy], [nc.vector.tensor_copy, nc.scalar.copy]]):
-            for t in range(PACK):
-                res = sb("res0_%d_%d" % (half, t), [P, HALF], F32)
-                copies[t % 2](out=res[:], in_=gradient(xi_mx, t, (half + 1) * HALF)[:, HALF:K])
-                nc.sync.dma_start(out=by_place(out_0)[:, t, half * HALF:(half + 1) * HALF], in_=res[:])
+        for c in range(2, PACK):
+            quantize(d_mx, E5M2, chunks(du_b, c), PACK + c)
+        store_out_0(0, [nc.scalar.copy, nc.scalar.copy], 2)
+        store_out_0(1, [nc.vector.tensor_copy, nc.scalar.copy], 1)

@@ -48,7 +48,7 @@ def tile_attend_gbpool_UV_kernel(tc, xT, dz, cf, si, U, eT, V, offs, out_0, out_
         si_col = load("si_col", si[0:1, :].rearrange("o (m r) -> m (o r)", r=PACK), nc.scalar)
         cf_col = load("cf_col", cf.rearrange("(p j) o -> p (j o)", j=PACK), nc.scalar)
         dz_raw = [load("dz_raw%d" % h, by_place(dz)[:, 2 * h:2 * h + 2, :]) for h in range(2)]
-        u_raw = [load("u_raw%d" % a, by_place(U)[:, :, a * HALF:(a + 1) * HALF]) for a in range(2)]
+        u_raw = load("u_raw", by_place(U))
         table = [load("table0", by_place(eT)[:, 0, :])]
         offsets = keep.tile([P, K // 16], U16, name="offsets")
         nc.sync.dma_start(offsets[:], offs)
@@ -118,12 +118,11 @@ def tile_attend_gbpool_UV_kernel(tc, xT, dz, cf, si, U, eT, V, offs, out_0, out_
                 nc.scalar.copy(out=res[:, e, :], in_=bank[:])
                 nc.sync.dma_start(out=by_place(out_1)[:, t + e, :], in_=res[:, e, :])
 
-        def store_out_0(half, copies, rows):
-            for t in range(0, PACK, rows):
-                res = sb("res0_%d_%d" % (half, t), [P, rows, HALF], F32)
-                for e in range(rows):
-                    copies[(t + e) % 2](out=res[:, e, :], in_=gradient(xi_mx, t + e, (half + 1) * HALF)[:, HALF:K])
-                nc.sync.dma_start(out=by_place(out_0)[:, t:t + rows, half * HALF:(half + 1) * HALF], in_=res[:])
+        def store_out_0(half, t, copies):
+            res = sb("res0_%d_%d" % (half, t), [P, len(copies), HALF], F32)
+            for e, copy in enumerate(copies):
+                copy(out=res[:, e, :], in_=gradient(xi_mx, t + e, (half + 1) * HALF)[:, HALF:K])
+            nc.sync.dma_start(out=by_place(out_0)[:, t:t + len(copies), half * HALF:(half + 1) * HALF], in_=res[:])
 
         x_d = sb("x_d", [P, PACK * K], BF16)
         x_d_view = x_d[:].rearrange("p (r m t) -> p m r t", r=PACK, t=PACK)
@@ -163,28 +162,29 @@ def tile_attend_gbpool_UV_kernel(tc, xT, dz, cf, si, U, eT, V, offs, out_0, out_
                 nc.tensor.transpose(bank[:, r, :], w[:, r * P:(r + 1) * P], ident[:])
             nc.scalar.copy(out=wT_view[:, :, j, :], in_=bank[:].rearrange("p r n -> p n r"))
 
-        u_b = sb("u_b", [P, PACK * K], BF16)
-        u_mx = mx_tiles("u", K)
+        u_b = [sb("u_b%d" % c, [P, K], BF16) for c in range(PACK)]
         dv_b = sb("dv_b", [P, PACK * K], BF16)
 
         def cast_u(c, copy):
-            cast_weights(chunks(u_b, c), u_raw[c // 2][:, :, (c % 2) * P:(c % 2 + 1) * P], copy)
+            cast_weights(u_b[c][:], u_raw[:, :, c * P:(c + 1) * P], copy)
 
-        def u_panel(c):
-            quantize(u_mx, E4M3, chunks(u_b, c), c)
-            return project(c, xd_mx, u_mx)
+        def u_panel(c, slot=None):
+            u_mx = mx_tiles("u%d" % c, P, slot)
+            quantize(u_mx, E4M3, u_b[c][:], 0)
+            return project(0, xd_mx, u_mx)
 
         for c in range(2):
             cast_u(c, nc.vector.tensor_copy)
-        u_banks = [u_panel(c) for c in range(2)]
-        xi_mx = mx_tiles("xi", K, "dz_raw1")
-        quantize(xi_mx, E4M3, x_i[:], 0)
+        u_banks = [u_panel(0)]
         cast_u(2, nc.vector.tensor_copy)
         cast_u(3, nc.scalar.copy)
-        for c in range(PACK):
+        u_banks.extend([u_panel(1), u_panel(2)])
+        xi_mx = mx_tiles("xi", K, "u_b1")
+        quantize(xi_mx, E4M3, x_i[:], 0)
+        weigh(u_banks[0], 0, chunks(dv_b, 0))
+        u_banks.append(u_panel(3, "u0_codes"))
+        for c in range(1, PACK):
             weigh(u_banks[c], c, chunks(dv_b, c))
-            if c < 2:
-                u_banks.append(u_panel(c + 2))
         d_mx = mx_tiles("d", 2 * K)
         for h in range(2):
             quantize(d_mx, E5M2, chunks(dv_b, 2 * h, 2), 2 * h)
@@ -263,5 +263,8 @@ def tile_attend_gbpool_UV_kernel(tc, xT, dz, cf, si, U, eT, V, offs, out_0, out_
             weigh(v_banks[c], c, chunks(du_b, c))
         for c in range(2, PACK):
             quantize(d_mx, E5M2, chunks(du_b, c), PACK + c)
-        store_out_0(0, [nc.scalar.copy, nc.scalar.copy], 2)
-        store_out_0(1, [nc.vector.tensor_copy, nc.scalar.copy], 1)
+        store_out_0(0, 0, [nc.scalar.copy, nc.scalar.copy])
+        store_out_0(0, 2, [nc.scalar.copy])
+        store_out_0(0, 3, [nc.scalar.copy])
+        for t in range(PACK):
+            store_out_0(1, t, [nc.scalar.copy if t % 2 else nc.vector.tensor_copy])

@@ -44,15 +44,17 @@ def tile_attend_gbpool_UV_kernel(tc, xT, dz, cf, si, U, eT, V, offs, out_0, out_
             queue.dma_start(out=tile[:], in_=src)
             return tile
 
-        x_raw = [load("x_raw%d" % h, by_place(xT)[:, 2 * h:2 * h + 2, :]) for h in range(2)]
         si_col = load("si_col", si[0:1, :].rearrange("o (m r) -> m (o r)", r=PACK), nc.scalar)
         cf_col = load("cf_col", cf.rearrange("(p j) o -> p (j o)", j=PACK), nc.scalar)
-        dz_raw = [load("dz_raw%d" % h, by_place(dz)[:, 2 * h:2 * h + 2, :]) for h in range(2)]
+        dz_raw, x_raw = [], []
+        for h in range(2):
+            x_raw.append(load("x_raw%d" % h, by_place(xT)[:, 2 * h:2 * h + 2, :]))
+            dz_raw.append(load("dz_raw%d" % h, by_place(dz)[:, 2 * h:2 * h + 2, :]))
         u_raw = load("u_raw", by_place(U))
-        table = [load("table0", by_place(eT)[:, 0, :])]
+        table0 = [load("table0_%d" % a, by_place(eT)[:, 0, a * ITEMS // 2:(a + 1) * ITEMS // 2]) for a in range(2)]
         offsets = keep.tile([P, K // 16], U16, name="offsets")
         nc.sync.dma_start(offsets[:], offs)
-        table.extend([load("table%d" % t, by_place(eT)[:, t, :]) for t in range(1, PACK)])
+        table = {t: load("table%d" % t, by_place(eT)[:, t, :]) for t in range(1, PACK)}
         v_raw = [load("v_raw%d" % c, by_place(V)[:, :, c * P:(c + 1) * P]) for c in range(PACK)]
 
         ones = sb("ones", [P, P], F32)
@@ -124,17 +126,19 @@ def tile_attend_gbpool_UV_kernel(tc, xT, dz, cf, si, U, eT, V, offs, out_0, out_
                 copy(out=res[:, e, :], in_=gradient(xi_mx, t + e, (half + 1) * HALF)[:, HALF:K])
             nc.sync.dma_start(out=by_place(out_0)[:, t:t + len(copies), half * HALF:(half + 1) * HALF], in_=res[:])
 
+        si_bank = new_bank([P, PACK, P])
+        for r in range(PACK):
+            nc.tensor.transpose(si_bank[:, r, :], si_col[:, r:r + 1].to_broadcast([P, P]), ident[:])
         x_d = sb("x_d", [P, PACK * K], BF16)
         x_d_view = x_d[:].rearrange("p (r m t) -> p m r t", r=PACK, t=PACK)
-        for h in range(2):
-            nc.vector.tensor_copy(out=x_d_view[:, :, :, 2 * h:2 * h + 2],
-                                  in_=x_raw[h][:].rearrange("p t (m r) -> p m r t", r=PACK))
-        xd_mx = mx_tiles("xd", K)
-        quantize(xd_mx, E4M3, x_d[:], 0)
         x_i = sb("x_i", [P, PACK * K], BF16)
         x_words = x_d[:].bitcast(F32)
+        wT = sb("wT", [P, PACK * K], F32)
+        wT_view = wT[:].rearrange("p (n j r) -> p n j r", j=PACK, r=PACK)
 
         def turn_x(h):
+            nc.vector.tensor_copy(out=x_d_view[:, :, :, 2 * h:2 * h + 2],
+                                  in_=x_raw[h][:].rearrange("p t (m r) -> p m r t", r=PACK))
             bank = new_bank([P, PACK, P])
             for r in range(PACK):
                 nc.tensor.transpose(bank[:, r, :], x_words[:, 2 * P * r + h:2 * P * (r + 1):2], ident[:])
@@ -142,15 +146,7 @@ def tile_attend_gbpool_UV_kernel(tc, xT, dz, cf, si, U, eT, V, offs, out_0, out_
             nc.scalar.copy(out=chunks(x_i, 2 * h, 2).rearrange("p (e n r) -> p e n r", e=2, r=PACK),
                            in_=halves.rearrange("p (r n e) -> p e n r", r=PACK, e=2))
 
-        turn_x(0)
-        si_bank = new_bank([P, PACK, P])
-        for r in range(PACK):
-            nc.tensor.transpose(si_bank[:, r, :], si_col[:, r:r + 1].to_broadcast([P, P]), ident[:])
-        turn_x(1)
-
-        wT = sb("wT", [P, PACK * K], F32)
-        wT_view = wT[:].rearrange("p (n j r) -> p n j r", j=PACK, r=PACK)
-        for j in range(PACK):
+        def turn_w(j):
             w = sb("w%d" % j, [P, K], F32)
             nc.vector.scalar_tensor_tensor(out=w[:].rearrange("p (r m) -> p m r", r=PACK),
                                            in0=dz_raw[j // 2][:, j % 2, :].rearrange("p (m r) -> p m r", r=PACK),
@@ -161,6 +157,13 @@ def tile_attend_gbpool_UV_kernel(tc, xT, dz, cf, si, U, eT, V, offs, out_0, out_
             for r in range(PACK):
                 nc.tensor.transpose(bank[:, r, :], w[:, r * P:(r + 1) * P], ident[:])
             nc.scalar.copy(out=wT_view[:, :, j, :], in_=bank[:].rearrange("p r n -> p n r"))
+
+        for h in range(2):
+            turn_x(h)
+            turn_w(2 * h)
+            turn_w(2 * h + 1)
+        xd_mx = mx_tiles("xd", K, "dz_raw1")
+        quantize(xd_mx, E4M3, x_d[:], 0)
 
         u_b = [sb("u_b%d" % c, [P, K], BF16) for c in range(PACK)]
         dv_b = sb("dv_b", [P, PACK * K], BF16)
@@ -209,7 +212,8 @@ def tile_attend_gbpool_UV_kernel(tc, xT, dz, cf, si, U, eT, V, offs, out_0, out_
             return gi_mx
 
         table0_b = sb("table0_b", [P, ITEMS], BF16)
-        nc.scalar.activation(out=table0_b[:], in_=table[0][:], func=COPY)
+        for a in range(2):
+            nc.scalar.activation(out=table0_b[:, a * ITEMS // 2:(a + 1) * ITEMS // 2], in_=table0[a][:], func=COPY)
         nc.scalar.activation(out=chunks(planes[0], 0), in_=table0_b[:].indirect(offsets[:]), func=COPY)
         gather(1, 0, K)
         g_i01 = sb("g_i01", [P, 2 * K], BF16)

@@ -49,7 +49,11 @@ def tile_attend_gbpool_UV_kernel(tc, xT, dz, cf, si, U, eT, V, offs, out_0, out_
         dz_raw, x_raw = [], []
         for h in range(2):
             x_raw.append(load("x_raw%d" % h, by_place(xT)[:, 2 * h:2 * h + 2, :]))
-            dz_raw.append(load("dz_raw%d" % h, by_place(dz)[:, 2 * h:2 * h + 2, :]))
+            if h == 0:
+                dz_pair = load("dz_raw01", by_place(dz)[:, 0:2, :])
+                dz_raw.extend([dz_pair[:, 0, :], dz_pair[:, 1, :]])
+            else:
+                dz_raw.extend([load("dz_raw%d" % j, by_place(dz)[:, j, :])[:] for j in range(2, PACK)])
         u_raw = load("u_raw", by_place(U))
         table0 = [load("table0_%d" % a, by_place(eT)[:, 0, a * ITEMS // 2:(a + 1) * ITEMS // 2]) for a in range(2)]
         offsets = keep.tile([P, K // 16], U16, name="offsets")
@@ -149,7 +153,7 @@ def tile_attend_gbpool_UV_kernel(tc, xT, dz, cf, si, U, eT, V, offs, out_0, out_
         def turn_w(j):
             w = sb("w%d" % j, [P, K], F32)
             nc.vector.scalar_tensor_tensor(out=w[:].rearrange("p (r m) -> p m r", r=PACK),
-                                           in0=dz_raw[j // 2][:, j % 2, :].rearrange("p (m r) -> p m r", r=PACK),
+                                           in0=dz_raw[j].rearrange("p (m r) -> p m r", r=PACK),
                                            scalar=cf_col[:, j:j + 1],
                                            in1=si_bank[:].rearrange("p r m -> p m r"),
                                            op0=ALU.mult, op1=ALU.mult)
@@ -162,7 +166,7 @@ def tile_attend_gbpool_UV_kernel(tc, xT, dz, cf, si, U, eT, V, offs, out_0, out_
             turn_x(h)
             turn_w(2 * h)
             turn_w(2 * h + 1)
-        xd_mx = mx_tiles("xd", K, "dz_raw1")
+        xd_mx = mx_tiles("xd", K, "dz_raw2")
         quantize(xd_mx, E4M3, x_d[:], 0)
 
         u_b = [sb("u_b%d" % c, [P, K], BF16) for c in range(PACK)]
@@ -242,8 +246,9 @@ def tile_attend_gbpool_UV_kernel(tc, xT, dz, cf, si, U, eT, V, offs, out_0, out_
         v_mx = mx_tiles("v", K)
         quantize(v_mx, E4M3, v_b[0], 0)
         ge_mx = mx_tiles("ge", K, "v_raw0")
-        for r in range(0, PACK, 2):
-            quantize(ge_mx, E4M3, chunks(g_e, r, 2), r)
+        quantize(ge_mx, E4M3, chunks(g_e, 0, 2), 0)
+        for r in range(2, PACK):
+            quantize(ge_mx, E4M3, chunks(g_e, r), r)
         v_banks = [project(0, ge_mx, v_mx)]
 
         def v_panel(c):

@@ -30,6 +30,9 @@ def tile_attend_gbpool_UV_kernel(tc, xT, dz, cf, si, U, eT, V, offs, out_0, out_
         def sb(name, shape, dtype, slot=None):
             return keep.tile(shape, dtype, name=name, tag=slot or name, align_bytes=64)
 
+        def rowed(name, n, dtype, slot=None):
+            return sb(name, [P, n * K], dtype, slot)[:].rearrange("p (t c) -> p t c", t=n)
+
         def new_bank(shape):
             return psum.tile(shape, F32, name="bank")
 
@@ -45,15 +48,9 @@ def tile_attend_gbpool_UV_kernel(tc, xT, dz, cf, si, U, eT, V, offs, out_0, out_
             return tile
 
         si_col = load("si_col", si[0:1, :].rearrange("o (m r) -> m (o r)", r=PACK), nc.scalar)
-        cf_col = load("cf_col", cf.rearrange("(p j) o -> p (j o)", j=PACK), nc.scalar)
-        dz_raw, x_raw = [], []
-        for h in range(2):
-            x_raw.append(load("x_raw%d" % h, by_place(xT)[:, 2 * h:2 * h + 2, :]))
-            if h == 0:
-                dz_pair = load("dz_raw01", by_place(dz)[:, 0:2, :])
-                dz_raw.extend([dz_pair[:, 0, :], dz_pair[:, 1, :]])
-            else:
-                dz_raw.extend([load("dz_raw%d" % j, by_place(dz)[:, j, :])[:] for j in range(2, PACK)])
+        cf_col = load("cf_col", cf.rearrange("(h p j) o -> p h (j o)", h=2, j=2), nc.scalar)
+        x_raw = [load("x_raw%d" % h, by_place(xT)[:, 2 * h:2 * h + 2, :]) for h in range(2)]
+        dz_raw = [load("dz_raw%d" % h, dz[h * HALF:(h + 1) * HALF, :].rearrange("(p j) i -> p j i", j=2)) for h in range(2)]
         u_raw = load("u_raw", by_place(U))
         table0 = [load("table0_%d" % a, by_place(eT)[:, 0, a * ITEMS // 2:(a + 1) * ITEMS // 2]) for a in range(2)]
         offsets = keep.tile([P, K // 16], U16, name="offsets")
@@ -94,8 +91,9 @@ def tile_attend_gbpool_UV_kernel(tc, xT, dz, cf, si, U, eT, V, offs, out_0, out_
             return bank
 
         def weigh(bank, c, dst):
-            nc.vector.tensor_tensor(out=dst.rearrange("p (n r) -> p n r", r=PACK), in0=bank[:].rearrange("p r n -> p n r"),
-                                    in1=chunks(wT, c).rearrange("p (n r) -> p n r", r=PACK), op=ALU.mult)
+            nc.vector.tensor_tensor(out=dst.rearrange("p (a b r) -> p a r b", b=4, r=PACK),
+                                    in0=bank[:].rearrange("p r (a b) -> p a r b", b=4),
+                                    in1=wT[:, :, c * P:(c + 1) * P].rearrange("p r (a b) -> p a r b", b=4), op=ALU.mult)
 
         def turn_planes(src):
             n = src.shape[1] // K
@@ -130,44 +128,41 @@ def tile_attend_gbpool_UV_kernel(tc, xT, dz, cf, si, U, eT, V, offs, out_0, out_
                 copy(out=res[:, e, :], in_=gradient(xi_mx, t + e, (half + 1) * HALF)[:, HALF:K])
             nc.sync.dma_start(out=by_place(out_0)[:, t:t + len(copies), half * HALF:(half + 1) * HALF], in_=res[:])
 
-        si_bank = new_bank([P, PACK, P])
-        for r in range(PACK):
-            nc.tensor.transpose(si_bank[:, r, :], si_col[:, r:r + 1].to_broadcast([P, P]), ident[:])
-        x_d = sb("x_d", [P, PACK * K], BF16)
-        x_d_view = x_d[:].rearrange("p (r m t) -> p m r t", r=PACK, t=PACK)
+        x_flat = sb("x_b", [P, PACK * K], BF16)
+        x_b = x_flat[:].rearrange("p (t c) -> p t c", t=PACK)
         x_i = sb("x_i", [P, PACK * K], BF16)
-        x_words = x_d[:].bitcast(F32)
-        wT = sb("wT", [P, PACK * K], F32)
-        wT_view = wT[:].rearrange("p (n j r) -> p n j r", j=PACK, r=PACK)
-
-        def turn_x(h):
-            nc.vector.tensor_copy(out=x_d_view[:, :, :, 2 * h:2 * h + 2],
-                                  in_=x_raw[h][:].rearrange("p t (m r) -> p m r t", r=PACK))
-            bank = new_bank([P, PACK, P])
-            for r in range(PACK):
-                nc.tensor.transpose(bank[:, r, :], x_words[:, 2 * P * r + h:2 * P * (r + 1):2], ident[:])
-            halves = bank[:].rearrange("p r n -> p (r n)").bitcast(BF16)
-            nc.scalar.copy(out=chunks(x_i, 2 * h, 2).rearrange("p (e n r) -> p e n r", e=2, r=PACK),
-                           in_=halves.rearrange("p (r n e) -> p e n r", r=PACK, e=2))
-
-        def turn_w(j):
-            w = sb("w%d" % j, [P, K], F32)
-            nc.vector.scalar_tensor_tensor(out=w[:].rearrange("p (r m) -> p m r", r=PACK),
-                                           in0=dz_raw[j].rearrange("p (m r) -> p m r", r=PACK),
-                                           scalar=cf_col[:, j:j + 1],
-                                           in1=si_bank[:].rearrange("p r m -> p m r"),
-                                           op0=ALU.mult, op1=ALU.mult)
-            bank = new_bank([P, PACK, P])
-            for r in range(PACK):
-                nc.tensor.transpose(bank[:, r, :], w[:, r * P:(r + 1) * P], ident[:])
-            nc.scalar.copy(out=wT_view[:, :, j, :], in_=bank[:].rearrange("p r n -> p n r"))
-
         for h in range(2):
-            turn_x(h)
-            turn_w(2 * h)
-            turn_w(2 * h + 1)
-        xd_mx = mx_tiles("xd", K, "dz_raw2")
+            nc.vector.tensor_copy(out=x_b[:, 2 * h:2 * h + 2, :], in_=x_raw[h][:])
+            weave_turned(turn_planes(chunks(x_flat, 2 * h, 2)), chunks(x_i, 2 * h, 2), nc.scalar.copy)
+        x_d = sb("x_d", [P, PACK * K], BF16)
+        nc.vector.tensor_copy(out=x_d[:].rearrange("p (r m t) -> p m t r", r=PACK, t=PACK),
+                              in_=x_b.rearrange("p t (m r) -> p m t r", r=PACK))
+
+        wT = rowed("wT", PACK, F32)
+
+        def turn_w(h):
+            w = rowed("w%d" % h, 2, F32)
+            for j in range(2):
+                nc.vector.tensor_scalar(out=w[:, j, :].rearrange("p (r m) -> p m r", r=PACK),
+                                        in0=dz_raw[h][:, j, :].rearrange("p (m r) -> p m r", r=PACK),
+                                        scalar1=cf_col[:, h, j:j + 1], scalar2=None, op0=ALU.mult)
+            for pair in range(2):
+                bank = new_bank([P, 2, 2, P])
+                for e in range(2):
+                    for j in range(2):
+                        r = 2 * pair + e
+                        nc.tensor.transpose(bank[:, e, j, :], w[:, j, r * P:(r + 1) * P], ident[:])
+                for e in range(2):
+                    r = 2 * pair + e
+                    nc.scalar.activation(out=wT[:, r, h * HALF:(h + 1) * HALF].rearrange("p (n j) -> p n j", j=2),
+                                         in_=bank[:, e].rearrange("p j n -> p n j"), func=COPY, scale=si_col[:, r:r + 1])
+
+        turn_w(0)
+        turn_w(1)
+        xd_mx = mx_tiles("xd", K)
         quantize(xd_mx, E4M3, x_d[:], 0)
+        xi_mx = mx_tiles("xi", K)
+        quantize(xi_mx, E4M3, x_i[:], 0)
 
         u_b = [sb("u_b%d" % c, [P, K], BF16) for c in range(PACK)]
         dv_b = sb("dv_b", [P, PACK * K], BF16)
@@ -184,17 +179,13 @@ def tile_attend_gbpool_UV_kernel(tc, xT, dz, cf, si, U, eT, V, offs, out_0, out_
             cast_u(c, nc.vector.tensor_copy)
         u_banks = [u_panel(0)]
         cast_u(2, nc.vector.tensor_copy)
-        cast_u(3, nc.scalar.copy)
-        u_banks.extend([u_panel(1), u_panel(2)])
-        xi_mx = mx_tiles("xi", K, "u_b1")
-        quantize(xi_mx, E4M3, x_i[:], 0)
+        u_banks.append(u_panel(1))
+        cast_u(3, nc.vector.tensor_copy)
+        u_banks.append(u_panel(2))
         weigh(u_banks[0], 0, chunks(dv_b, 0))
-        u_banks.append(u_panel(3, "u0_codes"))
+        u_banks.append(u_panel(3))
         for c in range(1, PACK):
             weigh(u_banks[c], c, chunks(dv_b, c))
-        d_mx = mx_tiles("d", 2 * K)
-        for h in range(2):
-            quantize(d_mx, E5M2, chunks(dv_b, 2 * h, 2), 2 * h)
 
         planes = [sb("planes%d" % h, [P, 2 * K], BF16) for h in range(2)]
         g_e = sb("g_e", [P, PACK * K], BF16)
@@ -220,6 +211,8 @@ def tile_attend_gbpool_UV_kernel(tc, xT, dz, cf, si, U, eT, V, offs, out_0, out_
             nc.scalar.activation(out=table0_b[:, a * ITEMS // 2:(a + 1) * ITEMS // 2], in_=table0[a][:], func=COPY)
         nc.scalar.activation(out=chunks(planes[0], 0), in_=table0_b[:].indirect(offsets[:]), func=COPY)
         gather(1, 0, K)
+        d_mx = mx_tiles("d", 2 * K, "table1")
+        quantize(d_mx, E5M2, dv_b[:], 0)
         g_i01 = sb("g_i01", [P, 2 * K], BF16)
         for t in range(2):
             weave_turned(turn_planes(chunks(planes[0], t)), chunks(g_i01, t), nc.scalar.copy)
@@ -272,8 +265,7 @@ def tile_attend_gbpool_UV_kernel(tc, xT, dz, cf, si, U, eT, V, offs, out_0, out_
             weigh(v_banks[c], c, chunks(du_b, c))
         for c in range(2, PACK):
             quantize(d_mx, E5M2, chunks(du_b, c), PACK + c)
-        store_out_0(0, 0, [nc.scalar.copy, nc.scalar.copy])
-        store_out_0(0, 2, [nc.scalar.copy])
-        store_out_0(0, 3, [nc.scalar.copy])
+        for t in range(PACK):
+            store_out_0(0, t, [nc.scalar.copy])
         for t in range(PACK):
             store_out_0(1, t, [nc.scalar.copy if t % 2 else nc.vector.tensor_copy])

@@ -70,6 +70,9 @@ def tile_attend_gbpool_UV_kernel(tc, xT, dz, cf, si, U, eT, V, offs, out_0, out_
             nc.vector.tensor_scalar(out=ident[rows, :], in0=ramp[rows, :], scalar1=ramp_turned[rows, q:q + 1],
                                     scalar2=None, op0=ALU.is_equal)
 
+        ident_b = sb("ident_b", [P, P], BF16)
+        nc.vector.tensor_copy(out=ident_b[:], in_=ident[:])
+
         def mx_tiles(name, width, slot=None):
             return sb(name + "_codes", [P, width], U32, slot), sb(name + "_scales", [P, width], U8)
 
@@ -115,6 +118,10 @@ def tile_attend_gbpool_UV_kernel(tc, xT, dz, cf, si, U, eT, V, offs, out_0, out_
             nc.tensor.matmul_mx(out=bank[:], lhsT=act_mx[0][:, cols].bitcast(E4M3), lhsT_scale=act_mx[1][:, cols],
                                 rhs=d_mx[0][:, window].bitcast(E5M2), rhs_scale=d_mx[1][:, window], start=True, stop=True)
             return bank
+
+        def cast_weights_on_gpsimd(dst, src):
+            nc.gpsimd.tensor_scalar(out=dst.rearrange("p (n t) -> p n t", t=PACK), in0=src.rearrange("p t n -> p n t"),
+                                    scalar1=1.0, scalar2=0.0, op0=ALU.mult, op1=ALU.add)
 
         def store_out_1(t, banks, slot=None):
             res = sb("res1_%d" % t, [P, len(banks), K], F32, slot)
@@ -187,19 +194,26 @@ def tile_attend_gbpool_UV_kernel(tc, xT, dz, cf, si, U, eT, V, offs, out_0, out_
         for c in range(1, PACK):
             weigh(u_banks[c], c, chunks(dv_b, c))
 
-        planes = [sb("planes%d" % h, [P, 2 * K], BF16) for h in range(2)]
+        planes = [sb("planes0", [P, 2 * K], BF16)]
         g_e = sb("g_e", [P, PACK * K], BF16)
         g_e_view = g_e[:].rearrange("p (r m t) -> p m r t", r=PACK, t=PACK)
-        pairs = [planes[h][:].rearrange("p (t m r) -> p m r t", t=2, r=PACK) for h in range(2)]
+        pairs = [planes[0][:].rearrange("p (t m r) -> p m r t", t=2, r=PACK)]
 
         def gather(t, first, count):
             nc.vector.tensor_copy(chunks(planes[t // 2], t % 2)[:, first:first + count],
                                   table[t][:].indirect(offsets[:, first // 16:(first + count) // 16]))
 
-        def turn(t):
-            g_i = sb("g_i%d" % t, [P, K], BF16)
-            weave_turned(turn_planes(chunks(planes[t // 2], t % 2)), g_i[:], nc.scalar.copy)
-            return g_i
+        def gather_into_place(t):
+            nc.vector.tensor_copy(g_e_view[:, :, :, t], table[t][:].indirect(offsets[:]))
+
+        def turn_place(t):
+            bank = psum.tile([P, PACK, P], BF16, name="bank")
+            for r in range(PACK):
+                nc.tensor.transpose(bank[:, r, :], g_e[:, r * K + t:(r + 1) * K:PACK], ident_b[:])
+            return bank
+
+        def weave_place(bank, g_i):
+            nc.scalar.copy(out=g_i[:].rearrange("p (n r) -> p n r", r=PACK), in_=bank[:].rearrange("p r n -> p n r"))
 
         def quantize_turned(t, g_i, slot=None):
             gi_mx = mx_tiles("gi%d" % t, P, slot)
@@ -219,24 +233,24 @@ def tile_attend_gbpool_UV_kernel(tc, xT, dz, cf, si, U, eT, V, offs, out_0, out_
         for a in range(2):
             nc.scalar.copy(out=g_e_view[:, :, 2 * a:2 * a + 2, 0:2].rearrange("p m r t -> p r m t"),
                            in_=pairs[0][:, :, 2 * a:2 * a + 2, :].rearrange("p m r t -> p r m t"))
-        gather(2, 0, K)
+        gather_into_place(2)
         gi01_mx = mx_tiles("gi01", 2 * P, "table2")
         quantize(gi01_mx, E4M3, g_i01[:], 0)
-        g_i2 = turn(2)
-        out_1_banks = [gradient(gi01_mx, t, 0) for t in range(2)]
-        for a in range(2):
-            gather(3, a * HALF, HALF)
-        for a in range(2):
-            nc.vector.tensor_copy(out=g_e_view[:, a * P // 2:(a + 1) * P // 2, :, 2:4], in_=pairs[1][:, a * P // 2:(a + 1) * P // 2])
-        g3_bank = turn_planes(chunks(planes[1], 1))
+        g_i2 = sb("g_i2", [P, K], BF16)
+        weave_place(turn_place(2), g_i2)
+        store_out_1(0, [gradient(gi01_mx, 0, 0)])
+        out_1_banks = [gradient(gi01_mx, 1, 0)]
+        gather_into_place(3)
+        g3_bank = turn_place(3)
 
         v_b = [sb("v_b%d" % c, [P, K], BF16)[:] for c in range(PACK)]
-        for c in range(PACK - 1):
+        cast_weights_on_gpsimd(v_b[0], v_raw[0][:])
+        for c in range(1, PACK - 1):
             cast_weights(v_b[c], v_raw[c][:], nc.scalar.copy)
         g_i3 = sb("g_i3", [P, K], BF16, "v_raw1")
-        weave_turned(g3_bank, g_i3[:], nc.scalar.copy)
+        weave_place(g3_bank, g_i3)
         cast_weights(v_b[PACK - 1], v_raw[PACK - 1][:], nc.scalar.copy)
-        v_mx = mx_tiles("v", K)
+        v_mx = mx_tiles("v0", P)
         quantize(v_mx, E4M3, v_b[0], 0)
         ge_mx = mx_tiles("ge", K, "v_raw0")
         quantize(ge_mx, E4M3, chunks(g_e, 0, 2), 0)
@@ -244,22 +258,23 @@ def tile_attend_gbpool_UV_kernel(tc, xT, dz, cf, si, U, eT, V, offs, out_0, out_
             quantize(ge_mx, E4M3, chunks(g_e, r), r)
         v_banks = [project(0, ge_mx, v_mx)]
 
-        def v_panel(c):
-            quantize(v_mx, E4M3, v_b[c], c)
-            return project(c, ge_mx, v_mx)
+        def v_panel(c, slot=None):
+            panel_mx = mx_tiles("v%d" % c, P, slot)
+            quantize(panel_mx, E4M3, v_b[c], 0)
+            return project(0, ge_mx, panel_mx)
 
         v_banks.append(v_panel(1))
         gi2_mx = quantize_turned(2, g_i2, "v_b0")
-        out_1_banks.append(gradient(gi2_mx, 0, 0))
         v_banks.append(v_panel(2))
+        out_1_banks.append(gradient(gi2_mx, 0, 0))
         du_b = sb("du_b", [P, PACK * K], BF16)
         weigh(v_banks[0], 0, chunks(du_b, 0))
         gi3_mx = quantize_turned(3, g_i3)
         out_1_banks.append(gradient(gi3_mx, 0, 0))
         weigh(v_banks[1], 1, chunks(du_b, 1))
-        store_out_1(0, out_1_banks, "v_raw3")
+        store_out_1(1, out_1_banks, "v_raw3")
         quantize(d_mx, E5M2, chunks(du_b, 0), PACK)
-        v_banks.append(v_panel(3))
+        v_banks.append(v_panel(3, "v1_codes"))
         quantize(d_mx, E5M2, chunks(du_b, 1), PACK + 1)
         for c in range(2, PACK):
             weigh(v_banks[c], c, chunks(du_b, c))

@@ -47,9 +47,12 @@ def tile_attend_gbpool_UV_kernel(tc, xT, dz, cf, si, U, eT, V, offs, out_0, out_
             queue.dma_start(out=tile[:], in_=src)
             return tile
 
-        si_col = load("si_col", si[0:1, :].rearrange("o (m r) -> m (o r)", r=PACK), nc.scalar)
-        cf_col = load("cf_col", cf.rearrange("(h p j) o -> p h (j o)", h=2, j=2), nc.scalar)
-        x_raw = [load("x_raw%d" % h, by_place(xT)[:, 2 * h:2 * h + 2, :]) for h in range(2)]
+        factors = sb("factors", [P, K], F32)
+        nc.vector.memset(factors[:], 0.0)
+        x_raw = [load("x_raw0", by_place(xT)[:, 0:2, :])]
+        nc.sync.dma_start(out=factors[0:1, :], in_=si[0:1, :])
+        nc.sync.dma_start(out=factors[1:2, :], in_=cf.rearrange("f o -> o f"))
+        x_raw.append(load("x_raw1", by_place(xT)[:, 2:PACK, :]))
         dz_raw = [load("dz_raw%d" % h, dz[h * HALF:(h + 1) * HALF, :].rearrange("(p j) i -> p j i", j=2)) for h in range(2)]
         u_raw = load("u_raw", by_place(U))
         table0 = [load("table0_%d" % a, by_place(eT)[:, 0, a * ITEMS // 2:(a + 1) * ITEMS // 2]) for a in range(2)]
@@ -70,6 +73,15 @@ def tile_attend_gbpool_UV_kernel(tc, xT, dz, cf, si, U, eT, V, offs, out_0, out_
             nc.vector.tensor_scalar(out=ident[rows, :], in0=ramp[rows, :], scalar1=ramp_turned[rows, q:q + 1],
                                     scalar2=None, op0=ALU.is_equal)
 
+        def factor_columns(name, row, columns):
+            bank = new_bank([P, PACK, P])
+            for n in range(PACK):
+                nc.tensor.transpose(bank[:, n, :], factors[:, columns[n]], ident[:])
+            col = sb(name, [P, PACK], F32)
+            nc.scalar.copy(out=col[:], in_=bank[:, :, row])
+            return col
+
+        cf_col = factor_columns("cf_col", 1, [slice(HALF * (n // 2) + n % 2, HALF * (n // 2 + 1), 2) for n in range(PACK)])
         ident_b = sb("ident_b", [P, P], BF16)
         nc.vector.tensor_copy(out=ident_b[:], in_=ident[:])
 
@@ -87,8 +99,9 @@ def tile_attend_gbpool_UV_kernel(tc, xT, dz, cf, si, U, eT, V, offs, out_0, out_
             bank = new_bank([P, PACK, P])
             cols = slice(c * P, (c + 1) * P)
             for r in range(PACK):
-                rc = slice(r * P, (r + 1) * P)
-                nc.tensor.matmul_mx(out=bank[:, r, :], lhsT=act_mx[0][:, rc].bitcast(E4M3), lhsT_scale=act_mx[1][:, rc],
+                codes, scales = act_mx[r // 2]
+                rc = slice(r % 2 * P, (r % 2 + 1) * P)
+                nc.tensor.matmul_mx(out=bank[:, r, :], lhsT=codes[:, rc].bitcast(E4M3), lhsT_scale=scales[:, rc],
                                     rhs=w_mx[0][:, cols].bitcast(E4M3), rhs_scale=w_mx[1][:, cols],
                                     start=True, stop=True)
             return bank
@@ -141,6 +154,7 @@ def tile_attend_gbpool_UV_kernel(tc, xT, dz, cf, si, U, eT, V, offs, out_0, out_
         for h in range(2):
             nc.vector.tensor_copy(out=x_b[:, 2 * h:2 * h + 2, :], in_=x_raw[h][:])
             weave_turned(turn_planes(chunks(x_flat, 2 * h, 2)), chunks(x_i, 2 * h, 2), nc.scalar.copy)
+        si_col = factor_columns("si_col", 0, [slice(r, K, PACK) for r in range(PACK)])
         x_d = sb("x_d", [P, PACK * K], BF16)
         nc.vector.tensor_copy(out=x_d[:].rearrange("p (r m t) -> p m t r", r=PACK, t=PACK),
                               in_=x_b.rearrange("p t (m r) -> p m t r", r=PACK))
@@ -152,7 +166,7 @@ def tile_attend_gbpool_UV_kernel(tc, xT, dz, cf, si, U, eT, V, offs, out_0, out_
             for j in range(2):
                 nc.vector.tensor_scalar(out=w[:, j, :].rearrange("p (r m) -> p m r", r=PACK),
                                         in0=dz_raw[h][:, j, :].rearrange("p (m r) -> p m r", r=PACK),
-                                        scalar1=cf_col[:, h, j:j + 1], scalar2=None, op0=ALU.mult)
+                                        scalar1=cf_col[:, 2 * h + j:2 * h + j + 1], scalar2=None, op0=ALU.mult)
             for pair in range(2):
                 bank = new_bank([P, 2, 2, P])
                 for e in range(2):
@@ -168,6 +182,7 @@ def tile_attend_gbpool_UV_kernel(tc, xT, dz, cf, si, U, eT, V, offs, out_0, out_
         turn_w(1)
         xd_mx = mx_tiles("xd", K)
         quantize(xd_mx, E4M3, x_d[:], 0)
+        xd_pairs = [(xd_mx[0][:, h * HALF:(h + 1) * HALF], xd_mx[1][:, h * HALF:(h + 1) * HALF]) for h in range(2)]
         xi_mx = mx_tiles("xi", K)
         quantize(xi_mx, E4M3, x_i[:], 0)
 
@@ -180,7 +195,7 @@ def tile_attend_gbpool_UV_kernel(tc, xT, dz, cf, si, U, eT, V, offs, out_0, out_
         def u_panel(c, slot=None):
             u_mx = mx_tiles("u%d" % c, P, slot)
             quantize(u_mx, E4M3, u_b[c][:], 0)
-            return project(0, xd_mx, u_mx)
+            return project(0, xd_pairs, u_mx)
 
         for c in range(2):
             cast_u(c, nc.vector.tensor_copy)
@@ -193,6 +208,10 @@ def tile_attend_gbpool_UV_kernel(tc, xT, dz, cf, si, U, eT, V, offs, out_0, out_
         u_banks.append(u_panel(3))
         for c in range(1, PACK):
             weigh(u_banks[c], c, chunks(dv_b, c))
+
+        d_mx = mx_tiles("d", 2 * K)
+        for h in range(2):
+            quantize(d_mx, E5M2, chunks(dv_b, 2 * h, 2), 2 * h)
 
         planes = [sb("planes0", [P, 2 * K], BF16)]
         g_e = sb("g_e", [P, PACK * K], BF16)
@@ -225,8 +244,6 @@ def tile_attend_gbpool_UV_kernel(tc, xT, dz, cf, si, U, eT, V, offs, out_0, out_
             nc.scalar.activation(out=table0_b[:, a * ITEMS // 2:(a + 1) * ITEMS // 2], in_=table0[a][:], func=COPY)
         nc.scalar.activation(out=chunks(planes[0], 0), in_=table0_b[:].indirect(offsets[:]), func=COPY)
         gather(1, 0, K)
-        d_mx = mx_tiles("d", 2 * K, "table1")
-        quantize(d_mx, E5M2, dv_b[:], 0)
         g_i01 = sb("g_i01", [P, 2 * K], BF16)
         for t in range(2):
             weave_turned(turn_planes(chunks(planes[0], t)), chunks(g_i01, t), nc.scalar.copy)
@@ -250,12 +267,12 @@ def tile_attend_gbpool_UV_kernel(tc, xT, dz, cf, si, U, eT, V, offs, out_0, out_
         g_i3 = sb("g_i3", [P, K], BF16, "v_raw1")
         weave_place(g3_bank, g_i3)
         cast_weights(v_b[PACK - 1], v_raw[PACK - 1][:], nc.scalar.copy)
+        ge_mx = [mx_tiles("ge01", HALF), mx_tiles("ge23", HALF, "v_raw0")]
+        quantize(ge_mx[0], E4M3, chunks(g_e, 0, 2), 0)
         v_mx = mx_tiles("v0", P)
         quantize(v_mx, E4M3, v_b[0], 0)
-        ge_mx = mx_tiles("ge", K, "v_raw0")
-        quantize(ge_mx, E4M3, chunks(g_e, 0, 2), 0)
         for r in range(2, PACK):
-            quantize(ge_mx, E4M3, chunks(g_e, r), r)
+            quantize(ge_mx[1], E4M3, chunks(g_e, r), r - 2)
         v_banks = [project(0, ge_mx, v_mx)]
 
         def v_panel(c, slot=None):
@@ -273,8 +290,8 @@ def tile_attend_gbpool_UV_kernel(tc, xT, dz, cf, si, U, eT, V, offs, out_0, out_
         out_1_banks.append(gradient(gi3_mx, 0, 0))
         weigh(v_banks[1], 1, chunks(du_b, 1))
         store_out_1(1, out_1_banks, "v_raw3")
-        quantize(d_mx, E5M2, chunks(du_b, 0), PACK)
         v_banks.append(v_panel(3, "v1_codes"))
+        quantize(d_mx, E5M2, chunks(du_b, 0), PACK)
         quantize(d_mx, E5M2, chunks(du_b, 1), PACK + 1)
         for c in range(2, PACK):
             weigh(v_banks[c], c, chunks(du_b, c))

@@ -82,6 +82,7 @@ def tile_attend_gbpool_UV_kernel(tc, xT, dz, cf, si, U, eT, V, offs, out_0, out_
             return col
 
         cf_col = factor_columns("cf_col", 1, [slice(HALF * (n // 2) + n % 2, HALF * (n // 2 + 1), 2) for n in range(PACK)])
+        si_col = factor_columns("si_col", 0, [slice(r, K, PACK) for r in range(PACK)])
         ident_b = sb("ident_b", [P, P], BF16)
         nc.vector.tensor_copy(out=ident_b[:], in_=ident[:])
 
@@ -154,19 +155,23 @@ def tile_attend_gbpool_UV_kernel(tc, xT, dz, cf, si, U, eT, V, offs, out_0, out_
         for h in range(2):
             nc.vector.tensor_copy(out=x_b[:, 2 * h:2 * h + 2, :], in_=x_raw[h][:])
             weave_turned(turn_planes(chunks(x_flat, 2 * h, 2)), chunks(x_i, 2 * h, 2), nc.scalar.copy)
-        si_col = factor_columns("si_col", 0, [slice(r, K, PACK) for r in range(PACK)])
         x_d = sb("x_d", [P, PACK * K], BF16)
         nc.vector.tensor_copy(out=x_d[:].rearrange("p (r m t) -> p m t r", r=PACK, t=PACK),
                               in_=x_b.rearrange("p t (m r) -> p m t r", r=PACK))
 
         wT = rowed("wT", PACK, F32)
 
-        def turn_w(h):
+        def scale_on_vector(out, in_, col):
+            nc.vector.tensor_scalar(out=out, in0=in_, scalar1=col, scalar2=None, op0=ALU.mult)
+
+        def scale_on_scalar(out, in_, col):
+            nc.scalar.activation(out=out, in_=in_, func=COPY, scale=col)
+
+        def turn_w(h, scale_rows):
             w = rowed("w%d" % h, 2, F32)
             for j in range(2):
-                nc.vector.tensor_scalar(out=w[:, j, :].rearrange("p (r m) -> p m r", r=PACK),
-                                        in0=dz_raw[h][:, j, :].rearrange("p (m r) -> p m r", r=PACK),
-                                        scalar1=cf_col[:, 2 * h + j:2 * h + j + 1], scalar2=None, op0=ALU.mult)
+                scale_rows(w[:, j, :].rearrange("p (r m) -> p m r", r=PACK),
+                           dz_raw[h][:, j, :].rearrange("p (m r) -> p m r", r=PACK), cf_col[:, 2 * h + j:2 * h + j + 1])
             for pair in range(2):
                 bank = new_bank([P, 2, 2, P])
                 for e in range(2):
@@ -178,8 +183,8 @@ def tile_attend_gbpool_UV_kernel(tc, xT, dz, cf, si, U, eT, V, offs, out_0, out_
                     nc.scalar.activation(out=wT[:, r, h * HALF:(h + 1) * HALF].rearrange("p (n j) -> p n j", j=2),
                                          in_=bank[:, e].rearrange("p j n -> p n j"), func=COPY, scale=si_col[:, r:r + 1])
 
-        turn_w(0)
-        turn_w(1)
+        turn_w(0, scale_on_vector)
+        turn_w(1, scale_on_scalar)
         xd_mx = mx_tiles("xd", K)
         quantize(xd_mx, E4M3, x_d[:], 0)
         xd_pairs = [(xd_mx[0][:, h * HALF:(h + 1) * HALF], xd_mx[1][:, h * HALF:(h + 1) * HALF]) for h in range(2)]

@@ -16,8 +16,10 @@ P = 128
 PACK = 4
 K = 512
 HALF = K // 2
-ITEMS = 2048
 QUADRANT = 32
+VECTOR_SHARE = 320
+TABLE2_AT = 4096
+V_AT = {0: 0, 2: 16384, 3: 24576}
 FLOPS = 4 * 2 * K * K * K
 
 
@@ -25,41 +27,45 @@ def tile_attend_gbpool_UV_kernel(tc, xT, dz, cf, si, U, eT, V, offs, out_0, out_
     nc = tc.nc
     with ExitStack() as ctx:
         keep = ctx.enter_context(tc.tile_pool(name="keep", bufs=1))
+        laid = ctx.enter_context(tc.tile_pool(name="laid", bufs=1))
         psum = ctx.enter_context(tc.psum_pool(name="psum", bufs=8))
 
         def sb(name, shape, dtype, slot=None):
             return keep.tile(shape, dtype, name=name, tag=slot or name, align_bytes=64)
 
-        def rowed(name, n, dtype, slot=None):
-            return sb(name, [P, n * K], dtype, slot)[:].rearrange("p (t c) -> p t c", t=n)
+        def at(offset, name, shape, dtype):
+            return laid.tile(shape, dtype, name=name, align_bytes=64, offset=offset)
 
         def new_bank(shape):
             return psum.tile(shape, F32, name="bank")
 
-        def chunks(ap, c, n=1):
+        def chunk(ap, c, n=1):
             return ap[:, c * K:(c + n) * K]
 
         def by_place(dram):
             return dram.rearrange("(p t) c -> p t c", t=PACK)
 
-        def load(name, src, queue=nc.sync):
-            tile = sb(name, src.shape, F32)
-            queue.dma_start(out=tile[:], in_=src)
+        def load(tile, src):
+            nc.sync.dma_start(out=tile[:], in_=src)
             return tile
+
+        def fetch(name, src):
+            return load(sb(name, src.shape, F32), src)
 
         factors = sb("factors", [P, K], F32)
         nc.vector.memset(factors[:], 0.0)
-        x_raw = [load("x_raw0", by_place(xT)[:, 0:2, :])]
+        x_raw = [fetch("x_raw0", by_place(xT)[:, 0:2, :])]
         nc.sync.dma_start(out=factors[0:1, :], in_=si[0:1, :])
         nc.sync.dma_start(out=factors[1:2, :], in_=cf.rearrange("f o -> o f"))
-        x_raw.append(load("x_raw1", by_place(xT)[:, 2:PACK, :]))
-        dz_raw = [load("dz_raw%d" % h, dz[h * HALF:(h + 1) * HALF, :].rearrange("(p j) i -> p j i", j=2)) for h in range(2)]
-        u_raw = load("u_raw", by_place(U))
-        table0 = [load("table0_%d" % a, by_place(eT)[:, 0, a * ITEMS // 2:(a + 1) * ITEMS // 2]) for a in range(2)]
+        x_raw.append(fetch("x_raw1", by_place(xT)[:, 2:PACK, :]))
+        dz_raw = fetch("dz_raw", by_place(dz))
+        u_raw = fetch("u_raw", by_place(U))
         offsets = keep.tile([P, K // 16], U16, name="offsets")
         nc.sync.dma_start(offsets[:], offs)
-        table = {t: load("table%d" % t, by_place(eT)[:, t, :]) for t in range(1, PACK)}
-        v_raw = [load("v_raw%d" % c, by_place(V)[:, :, c * P:(c + 1) * P]) for c in range(PACK)]
+        table = [fetch("table%d" % t, by_place(eT)[:, t, :]) if t != 2 else
+                 load(at(TABLE2_AT, "table2", [P, 4 * K], F32), by_place(eT)[:, t, :]) for t in range(PACK)]
+        v_raw = [load(at(V_AT[c], "v_raw%d" % c, [P, PACK, P], F32) if c in V_AT else sb("v_raw%d" % c, [P, PACK, P], F32),
+                      by_place(V)[:, :, c * P:(c + 1) * P]) for c in range(PACK)]
 
         ones = sb("ones", [P, P], F32)
         nc.vector.memset(ones[:], 1.0)
@@ -73,46 +79,46 @@ def tile_attend_gbpool_UV_kernel(tc, xT, dz, cf, si, U, eT, V, offs, out_0, out_
             nc.vector.tensor_scalar(out=ident[rows, :], in0=ramp[rows, :], scalar1=ramp_turned[rows, q:q + 1],
                                     scalar2=None, op0=ALU.is_equal)
 
-        def factor_columns(name, row, columns):
-            bank = new_bank([P, PACK, P])
-            for n in range(PACK):
-                nc.tensor.transpose(bank[:, n, :], factors[:, columns[n]], ident[:])
-            col = sb(name, [P, PACK], F32)
-            nc.scalar.copy(out=col[:], in_=bank[:, :, row])
-            return col
-
-        cf_col = factor_columns("cf_col", 1, [slice(HALF * (n // 2) + n % 2, HALF * (n // 2 + 1), 2) for n in range(PACK)])
-        si_col = factor_columns("si_col", 0, [slice(r, K, PACK) for r in range(PACK)])
-        ident_b = sb("ident_b", [P, P], BF16)
-        nc.vector.tensor_copy(out=ident_b[:], in_=ident[:])
+        factor_bank = new_bank([P, PACK, P])
+        for r in range(PACK):
+            nc.tensor.transpose(factor_bank[:, r, :], factors[:, r:K:PACK], ident[:])
+        factor_cols = sb("factor_cols", [P, PACK, 2], F32)
+        nc.scalar.copy(out=factor_cols[:], in_=factor_bank[:, :, 0:2])
 
         def mx_tiles(name, width, slot=None):
             return sb(name + "_codes", [P, width], U32, slot), sb(name + "_scales", [P, width], U8)
 
-        def quantize(mx, fmt, src, c):
-            cols = slice(c * P, c * P + src.shape[1] // PACK)
+        def quantize(mx, fmt, src, first=0):
+            cols = slice(first, first + src.shape[1] // PACK)
             nc.vector.quantize_mx(out=mx[0][:, cols].bitcast(fmt), scales=mx[1][:, cols], in_=src)
 
-        def cast_weights(dst, src, copy):
+        def product(out, still, still_first, moving, moving_cols, fmt):
+            cols = slice(still_first, still_first + P)
+            nc.tensor.matmul_mx(out=out, lhsT=still[0][:, cols].bitcast(E4M3), lhsT_scale=still[1][:, cols],
+                                rhs=moving[0][:, moving_cols].bitcast(fmt), rhs_scale=moving[1][:, moving_cols],
+                                start=True, stop=True)
+
+        def round_panel(dst, src, copy):
             copy(out=dst.rearrange("p (a b t) -> p a t b", b=4, t=PACK), in_=src.rearrange("p t (a b) -> p a t b", b=4))
 
-        def project(c, act_mx, w_mx):
+        def project(name, rounded, pairs, slot=None):
+            panel = mx_tiles(name, P, slot)
+            quantize(panel, E4M3, rounded)
+            return lambda: projected(panel, pairs)
+
+        def projected(panel, pairs):
             bank = new_bank([P, PACK, P])
-            cols = slice(c * P, (c + 1) * P)
             for r in range(PACK):
-                codes, scales = act_mx[r // 2]
-                rc = slice(r % 2 * P, (r % 2 + 1) * P)
-                nc.tensor.matmul_mx(out=bank[:, r, :], lhsT=codes[:, rc].bitcast(E4M3), lhsT_scale=scales[:, rc],
-                                    rhs=w_mx[0][:, cols].bitcast(E4M3), rhs_scale=w_mx[1][:, cols],
-                                    start=True, stop=True)
+                product(bank[:, r, :], pairs[r // 2], r % 2 * P, panel, slice(0, P), E4M3)
             return bank
 
         def weigh(bank, c, dst):
             nc.vector.tensor_tensor(out=dst.rearrange("p (a b r) -> p a r b", b=4, r=PACK),
                                     in0=bank[:].rearrange("p r (a b) -> p a r b", b=4),
-                                    in1=wT[:, :, c * P:(c + 1) * P].rearrange("p r (a b) -> p a r b", b=4), op=ALU.mult)
+                                    in1=weight[:, :, c * P:(c + 1) * P].rearrange("p r (a b) -> p a r b", b=4),
+                                    op=ALU.mult)
 
-        def turn_planes(src):
+        def turn(src):
             n = src.shape[1] // K
             words = src.bitcast(F32)
             bank = new_bank([P, 2 * n, P])
@@ -121,188 +127,150 @@ def tile_attend_gbpool_UV_kernel(tc, xT, dz, cf, si, U, eT, V, offs, out_0, out_
                     nc.tensor.transpose(bank[:, 2 * e + u, :], words[:, 2 * P * e + u:2 * P * (e + 1):2], ident[:])
             return bank
 
-        def weave_turned(bank, dst, copy):
-            copy(out=dst.bitcast(F32).rearrange("p (e n u) -> p e n u", n=P, u=2),
-                 in_=bank[:].rearrange("p (e u) n -> p e n u", u=2))
+        def copy_turned(bank, dst):
+            nc.scalar.copy(out=dst.bitcast(F32).rearrange("p (e n u) -> p e n u", n=P, u=2),
+                           in_=bank[:].rearrange("p (e u) n -> p e n u", u=2))
 
-        def gradient(act_mx, c, first):
-            bank = new_bank([P, K])
-            cols = slice(c * P, (c + 1) * P)
-            window = slice(first, first + K)
-            nc.tensor.matmul_mx(out=bank[:], lhsT=act_mx[0][:, cols].bitcast(E4M3), lhsT_scale=act_mx[1][:, cols],
-                                rhs=d_mx[0][:, window].bitcast(E5M2), rhs_scale=d_mx[1][:, window], start=True, stop=True)
-            return bank
-
-        def cast_weights_on_gpsimd(dst, src):
-            nc.gpsimd.tensor_scalar(out=dst.rearrange("p (n t) -> p n t", t=PACK), in0=src.rearrange("p t n -> p n t"),
-                                    scalar1=1.0, scalar2=0.0, op0=ALU.mult, op1=ALU.add)
-
-        def store_out_1(t, banks, slot=None):
-            res = sb("res1_%d" % t, [P, len(banks), K], F32, slot)
-            for e, bank in enumerate(banks):
-                nc.scalar.copy(out=res[:, e, :], in_=bank[:])
-                nc.sync.dma_start(out=by_place(out_1)[:, t + e, :], in_=res[:, e, :])
-
-        def store_out_0(half, t, copies):
-            res = sb("res0_%d_%d" % (half, t), [P, len(copies), HALF], F32)
-            for e, copy in enumerate(copies):
-                copy(out=res[:, e, :], in_=gradient(xi_mx, t + e, (half + 1) * HALF)[:, HALF:K])
-            nc.sync.dma_start(out=by_place(out_0)[:, t:t + len(copies), half * HALF:(half + 1) * HALF], in_=res[:])
-
-        x_flat = sb("x_b", [P, PACK * K], BF16)
-        x_b = x_flat[:].rearrange("p (t c) -> p t c", t=PACK)
+        x_b = sb("x_b", [P, PACK * K], BF16)
         x_i = sb("x_i", [P, PACK * K], BF16)
         for h in range(2):
-            nc.vector.tensor_copy(out=x_b[:, 2 * h:2 * h + 2, :], in_=x_raw[h][:])
-            weave_turned(turn_planes(chunks(x_flat, 2 * h, 2)), chunks(x_i, 2 * h, 2), nc.scalar.copy)
+            nc.vector.tensor_copy(out=chunk(x_b, 2 * h, 2), in_=x_raw[h][:].rearrange("p t c -> p (t c)"))
+            copy_turned(turn(chunk(x_b, 2 * h, 2)), chunk(x_i, 2 * h, 2))
         x_d = sb("x_d", [P, PACK * K], BF16)
         nc.vector.tensor_copy(out=x_d[:].rearrange("p (r m t) -> p m t r", r=PACK, t=PACK),
-                              in_=x_b.rearrange("p t (m r) -> p m t r", r=PACK))
+                              in_=x_b[:].rearrange("p (t m r) -> p m t r", t=PACK, r=PACK))
 
-        wT = rowed("wT", PACK, F32)
+        scaled = sb("scaled", [P, PACK * K], F32)
+        weight = sb("weight", [P, PACK * K], F32)[:].rearrange("p (r c) -> p r c", r=PACK)
+        for j in range(PACK):
+            dealt = chunk(scaled, j).rearrange("p (r m) -> p m r", r=PACK)
+            row = dz_raw[:, j, :].rearrange("p (m r) -> p m r", r=PACK)
+            if j < 2:
+                nc.vector.tensor_scalar(out=dealt, in0=row, scalar1=factor_cols[:, j, 1:2], scalar2=None, op0=ALU.mult)
+            else:
+                nc.scalar.activation(out=dealt, in_=row, func=COPY, scale=factor_cols[:, j, 1:2])
+        for r in range(PACK):
+            bank = new_bank([P, PACK, P])
+            for j in range(PACK):
+                nc.tensor.transpose(bank[:, j, :], chunk(scaled, j)[:, r * P:(r + 1) * P], ident[:])
+            nc.scalar.activation(out=weight[:, r, :].rearrange("p (n j) -> p n j", j=PACK),
+                                 in_=bank[:].rearrange("p j n -> p n j"), func=COPY, scale=factor_cols[:, r, 0:1])
 
-        def scale_on_vector(out, in_, col):
-            nc.vector.tensor_scalar(out=out, in0=in_, scalar1=col, scalar2=None, op0=ALU.mult)
-
-        def scale_on_scalar(out, in_, col):
-            nc.scalar.activation(out=out, in_=in_, func=COPY, scale=col)
-
-        def turn_w(h, scale_rows):
-            w = rowed("w%d" % h, 2, F32)
-            for j in range(2):
-                scale_rows(w[:, j, :].rearrange("p (r m) -> p m r", r=PACK),
-                           dz_raw[h][:, j, :].rearrange("p (m r) -> p m r", r=PACK), cf_col[:, 2 * h + j:2 * h + j + 1])
-            for pair in range(2):
-                bank = new_bank([P, 2, 2, P])
-                for e in range(2):
-                    for j in range(2):
-                        r = 2 * pair + e
-                        nc.tensor.transpose(bank[:, e, j, :], w[:, j, r * P:(r + 1) * P], ident[:])
-                for e in range(2):
-                    r = 2 * pair + e
-                    nc.scalar.activation(out=wT[:, r, h * HALF:(h + 1) * HALF].rearrange("p (n j) -> p n j", j=2),
-                                         in_=bank[:, e].rearrange("p j n -> p n j"), func=COPY, scale=si_col[:, r:r + 1])
-
-        turn_w(0, scale_on_vector)
-        turn_w(1, scale_on_scalar)
         xd_mx = mx_tiles("xd", K)
-        quantize(xd_mx, E4M3, x_d[:], 0)
-        xd_pairs = [(xd_mx[0][:, h * HALF:(h + 1) * HALF], xd_mx[1][:, h * HALF:(h + 1) * HALF]) for h in range(2)]
-        xi_mx = mx_tiles("xi", K)
-        quantize(xi_mx, E4M3, x_i[:], 0)
+        quantize(xd_mx, E4M3, x_d[:])
+        xd_pairs = [[part[:, h * HALF:(h + 1) * HALF] for part in xd_mx] for h in range(2)]
+        xi_mx = mx_tiles("xi", K, "dz_raw")
+        quantize(xi_mx, E4M3, x_i[:])
 
-        u_b = [sb("u_b%d" % c, [P, K], BF16) for c in range(PACK)]
+        u_b = sb("u_b", [P, PACK * K], BF16)
+        u_banks = []
+        round_panel(chunk(u_b, 0), u_raw[:, :, 0:P], nc.vector.tensor_copy)
+        for c in range(PACK):
+            if c + 1 < PACK:
+                round_panel(chunk(u_b, c + 1), u_raw[:, :, (c + 1) * P:(c + 2) * P], nc.vector.tensor_copy)
+            u_banks.append(project("u%d" % c, chunk(u_b, c), xd_pairs)())
         dv_b = sb("dv_b", [P, PACK * K], BF16)
-
-        def cast_u(c, copy):
-            cast_weights(u_b[c][:], u_raw[:, :, c * P:(c + 1) * P], copy)
-
-        def u_panel(c, slot=None):
-            u_mx = mx_tiles("u%d" % c, P, slot)
-            quantize(u_mx, E4M3, u_b[c][:], 0)
-            return project(0, xd_pairs, u_mx)
-
-        for c in range(2):
-            cast_u(c, nc.vector.tensor_copy)
-        u_banks = [u_panel(0)]
-        cast_u(2, nc.vector.tensor_copy)
-        u_banks.append(u_panel(1))
-        cast_u(3, nc.vector.tensor_copy)
-        u_banks.append(u_panel(2))
-        weigh(u_banks[0], 0, chunks(dv_b, 0))
-        u_banks.append(u_panel(3))
-        for c in range(1, PACK):
-            weigh(u_banks[c], c, chunks(dv_b, c))
-
-        d_mx = mx_tiles("d", 2 * K)
+        for c in range(PACK):
+            weigh(u_banks[c], c, chunk(dv_b, c))
+        dv_mx = mx_tiles("dv", K)
         for h in range(2):
-            quantize(d_mx, E5M2, chunks(dv_b, 2 * h, 2), 2 * h)
+            quantize(dv_mx, E5M2, chunk(dv_b, 2 * h, 2), h * HALF)
 
-        planes = [sb("planes0", [P, 2 * K], BF16)]
-        g_e = sb("g_e", [P, PACK * K], BF16)
-        g_e_view = g_e[:].rearrange("p (r m t) -> p m r t", r=PACK, t=PACK)
-        pairs = [planes[0][:].rearrange("p (t m r) -> p m r t", t=2, r=PACK)]
+        pair = [sb("pair%d" % h, [P, 2 * K], BF16) for h in range(2)]
+        g_e = [sb("g_e0", [P, 2 * K], BF16)]
 
-        def gather(t, first, count):
-            nc.vector.tensor_copy(chunks(planes[t // 2], t % 2)[:, first:first + count],
-                                  table[t][:].indirect(offsets[:, first // 16:(first + count) // 16]))
+        def plane(t):
+            return chunk(pair[t // 2], t % 2)
 
-        def gather_into_place(t):
-            nc.vector.tensor_copy(g_e_view[:, :, :, t], table[t][:].indirect(offsets[:]))
+        def gather_on_vector(t, first, last):
+            nc.vector.tensor_copy(plane(t)[:, first:last], table[t][:].indirect(offsets[:, first // 16:last // 16]))
 
-        def turn_place(t):
-            bank = psum.tile([P, PACK, P], BF16, name="bank")
-            for r in range(PACK):
-                nc.tensor.transpose(bank[:, r, :], g_e[:, r * K + t:(r + 1) * K:PACK], ident_b[:])
-            return bank
+        def gather_on_scalar(t, first, last):
+            nc.scalar.activation(out=plane(t)[:, first:last],
+                                 in_=table[t][:].indirect(offsets[:, first // 16:last // 16]), func=COPY)
 
-        def weave_place(bank, g_i):
-            nc.scalar.copy(out=g_i[:].rearrange("p (n r) -> p n r", r=PACK), in_=bank[:].rearrange("p r n -> p n r"))
+        def lay_pair(h, a, copy):
+            copy(out=g_e[a][:].rearrange("p (r m t) -> p r m t", r=2, t=PACK)[:, :, :, 2 * h:2 * h + 2],
+                 in_=pair[h][:].rearrange("p (t m r) -> p r m t", t=2, r=PACK)[:, 2 * a:2 * a + 2])
 
-        def quantize_turned(t, g_i, slot=None):
+        def along_i(t, g_i, slot=None):
             gi_mx = mx_tiles("gi%d" % t, P, slot)
-            quantize(gi_mx, E4M3, g_i[:], 0)
+            quantize(gi_mx, E4M3, g_i)
             return gi_mx
 
-        table0_b = sb("table0_b", [P, ITEMS], BF16)
-        for a in range(2):
-            nc.scalar.activation(out=table0_b[:, a * ITEMS // 2:(a + 1) * ITEMS // 2], in_=table0[a][:], func=COPY)
-        nc.scalar.activation(out=chunks(planes[0], 0), in_=table0_b[:].indirect(offsets[:]), func=COPY)
-        gather(1, 0, K)
-        g_i01 = sb("g_i01", [P, 2 * K], BF16)
+        def out_1_bank(gi_mx):
+            bank = new_bank([P, K])
+            product(bank[:], gi_mx, 0, dv_mx, slice(0, K), E5M2)
+            return bank
+
+        def store_out_1(t, bank, res):
+            nc.scalar.copy(out=res, in_=bank[:])
+            nc.sync.dma_start(out=by_place(out_1)[:, t, :], in_=res)
+
+        g_i = sb("g_i", [P, (PACK - 1) * K], BF16)
         for t in range(2):
-            weave_turned(turn_planes(chunks(planes[0], t)), chunks(g_i01, t), nc.scalar.copy)
+            gather_on_scalar(t, 0, K)
+        turned = [turn(plane(t)) for t in range(2)]
+        for t in range(2):
+            copy_turned(turned[t], chunk(g_i, t))
+        first_bank = out_1_bank(along_i(0, chunk(g_i, 0)))
+        lay_pair(0, 0, nc.vector.tensor_copy)
+        gather_on_vector(2, 0, VECTOR_SHARE)
+        gather_on_scalar(2, VECTOR_SHARE, K)
+        store_out_1(0, first_bank, at(TABLE2_AT + 8 * K, "res1_0", [P, K], F32)[:])
+        gi1_mx = at(TABLE2_AT, "gi1_codes", [P, P], U32), sb("gi1_scales", [P, P], U8)
+        quantize(gi1_mx, E4M3, chunk(g_i, 1))
+        g_e.append(at(TABLE2_AT + 2 * K, "g_e1", [P, 2 * K], BF16))
+        lay_pair(0, 1, nc.vector.tensor_copy)
+        copy_turned(turn(plane(2)), chunk(g_i, 2))
+
+        gather_on_vector(3, 0, VECTOR_SHARE)
+        gather_on_scalar(3, VECTOR_SHARE, K)
+        last_turned = turn(plane(3))
+        gi2_mx = along_i(2, chunk(g_i, 2), "table3")
+        second_bank = out_1_bank(gi1_mx)
+        late_banks = [out_1_bank(gi2_mx)]
         for a in range(2):
-            nc.scalar.copy(out=g_e_view[:, :, 2 * a:2 * a + 2, 0:2].rearrange("p m r t -> p r m t"),
-                           in_=pairs[0][:, :, 2 * a:2 * a + 2, :].rearrange("p m r t -> p r m t"))
-        gather_into_place(2)
-        gi01_mx = mx_tiles("gi01", 2 * P, "table2")
-        quantize(gi01_mx, E4M3, g_i01[:], 0)
-        g_i2 = sb("g_i2", [P, K], BF16)
-        weave_place(turn_place(2), g_i2)
-        store_out_1(0, [gradient(gi01_mx, 0, 0)])
-        out_1_banks = [gradient(gi01_mx, 1, 0)]
-        gather_into_place(3)
-        g3_bank = turn_place(3)
+            lay_pair(1, a, nc.vector.tensor_copy)
 
         v_b = [sb("v_b%d" % c, [P, K], BF16)[:] for c in range(PACK)]
-        cast_weights_on_gpsimd(v_b[0], v_raw[0][:])
-        for c in range(1, PACK - 1):
-            cast_weights(v_b[c], v_raw[c][:], nc.scalar.copy)
-        g_i3 = sb("g_i3", [P, K], BF16, "v_raw1")
-        weave_place(g3_bank, g_i3)
-        cast_weights(v_b[PACK - 1], v_raw[PACK - 1][:], nc.scalar.copy)
-        ge_mx = [mx_tiles("ge01", HALF), mx_tiles("ge23", HALF, "v_raw0")]
-        quantize(ge_mx[0], E4M3, chunks(g_e, 0, 2), 0)
-        v_mx = mx_tiles("v0", P)
-        quantize(v_mx, E4M3, v_b[0], 0)
+        round_panel(v_b[0], v_raw[0][:], nc.scalar.copy)
+        g_i3 = at(V_AT[0] + 2 * K, "g_i3", [P, K], BF16)
+        copy_turned(last_turned, g_i3[:])
+        for c in range(1, 3):
+            round_panel(v_b[c], v_raw[c][:], nc.scalar.copy)
+        store_out_1(1, second_bank, at(V_AT[2] + 2 * K, "res1_1", [P, K], F32)[:])
+        round_panel(v_b[3], v_raw[3][:], nc.scalar.copy)
+
+        ge_pairs = [mx_tiles("ge01", HALF), (at(0, "ge23_codes", [P, HALF], U32), sb("ge23_scales", [P, HALF], U8))]
+        quantize(ge_pairs[0], E4M3, g_e[0][:])
+        first_panel = project("v0", v_b[0], ge_pairs)
         for r in range(2, PACK):
-            quantize(ge_mx[1], E4M3, chunks(g_e, r), r - 2)
-        v_banks = [project(0, ge_mx, v_mx)]
-
-        def v_panel(c, slot=None):
-            panel_mx = mx_tiles("v%d" % c, P, slot)
-            quantize(panel_mx, E4M3, v_b[c], 0)
-            return project(0, ge_mx, panel_mx)
-
-        v_banks.append(v_panel(1))
-        gi2_mx = quantize_turned(2, g_i2, "v_b0")
-        v_banks.append(v_panel(2))
-        out_1_banks.append(gradient(gi2_mx, 0, 0))
-        du_b = sb("du_b", [P, PACK * K], BF16)
-        weigh(v_banks[0], 0, chunks(du_b, 0))
-        gi3_mx = quantize_turned(3, g_i3)
-        out_1_banks.append(gradient(gi3_mx, 0, 0))
-        weigh(v_banks[1], 1, chunks(du_b, 1))
-        store_out_1(1, out_1_banks, "v_raw3")
-        v_banks.append(v_panel(3, "v1_codes"))
-        quantize(d_mx, E5M2, chunks(du_b, 0), PACK)
-        quantize(d_mx, E5M2, chunks(du_b, 1), PACK + 1)
+            quantize(ge_pairs[1], E4M3, chunk(g_e[1], r - 2), (r - 2) * P)
+        v_banks = [first_panel()]
+        v_banks.append(project("v1", v_b[1], ge_pairs)())
+        late_banks.append(out_1_bank(along_i(3, g_i3[:])))
+        v_banks.append(project("v2", v_b[2], ge_pairs)())
+        du_b = [at(V_AT[2] - 2 * K, "du_b0", [P, 2 * K], BF16), at(V_AT[3] - 3 * K, "du_b1", [P, 2 * K], BF16)]
+        for c in range(2):
+            weigh(v_banks[c], c, chunk(du_b[0], c))
+        late_res = at(V_AT[3] + 2 * K, "res1_23", [P, 2, K], F32)
+        for e in range(2):
+            store_out_1(2 + e, late_banks[e], late_res[:, e, :])
+        v_banks.append(project("v3", v_b[3], ge_pairs)())
+        du_mx = sb("du_codes", [P, K], U32), at(V_AT[3] + K, "du_scales", [P, K], U8)
+        for c in range(2):
+            quantize(du_mx, E5M2, chunk(du_b[0], c), c * P)
         for c in range(2, PACK):
-            weigh(v_banks[c], c, chunks(du_b, c))
+            weigh(v_banks[c], c, chunk(du_b[1], c - 2))
         for c in range(2, PACK):
-            quantize(d_mx, E5M2, chunks(du_b, c), PACK + c)
-        for t in range(PACK):
-            store_out_0(0, t, [nc.scalar.copy])
-        for t in range(PACK):
-            store_out_0(1, t, [nc.scalar.copy if t % 2 else nc.vector.tensor_copy])
+            quantize(du_mx, E5M2, chunk(du_b[1], c - 2), c * P)
+        for h in range(2):
+            cols = slice(h * HALF, (h + 1) * HALF)
+            for t in range(PACK):
+                bank = new_bank([P, HALF])
+                product(bank[:], xi_mx, t * P, du_mx, cols, E5M2)
+                res = sb("res0_%d_%d" % (h, t), [P, HALF], F32)
+                copy = nc.vector.tensor_copy if h == 1 and t % 2 == 0 else nc.scalar.copy
+                copy(out=res[:], in_=bank[:])
+                nc.sync.dma_start(out=by_place(out_0)[:, t, cols], in_=res[:])

@@ -17,7 +17,7 @@ PACK = 4
 K = 512
 HALF = K // 2
 QUADRANT = 32
-VECTOR_SHARE = 320
+VECTOR_SHARE = 256
 TABLE2_AT = 4096
 V_AT = {0: 0, 2: 16384, 3: 24576}
 FLOPS = 4 * 2 * K * K * K
@@ -177,7 +177,6 @@ def tile_attend_gbpool_UV_kernel(tc, xT, dz, cf, si, U, eT, V, offs, out_0, out_
             quantize(dv_mx, E5M2, chunk(dv_b, 2 * h, 2), h * HALF)
 
         pair = [sb("pair%d" % h, [P, 2 * K], BF16) for h in range(2)]
-        g_e = [sb("g_e0", [P, 2 * K], BF16)]
 
         def plane(t):
             return chunk(pair[t // 2], t % 2)
@@ -189,9 +188,10 @@ def tile_attend_gbpool_UV_kernel(tc, xT, dz, cf, si, U, eT, V, offs, out_0, out_
             nc.scalar.activation(out=plane(t)[:, first:last],
                                  in_=table[t][:].indirect(offsets[:, first // 16:last // 16]), func=COPY)
 
-        def lay_pair(h, a, copy):
-            copy(out=g_e[a][:].rearrange("p (r m t) -> p r m t", r=2, t=PACK)[:, :, :, 2 * h:2 * h + 2],
-                 in_=pair[h][:].rearrange("p (t m r) -> p r m t", t=2, r=PACK)[:, 2 * a:2 * a + 2])
+        def lay_pair(h, first, last, copy):
+            rows = slice(first // PACK, last // PACK)
+            copy(out=g_e[:].rearrange("p (r m t) -> p r m t", r=PACK, t=PACK)[:, :, rows, 2 * h:2 * h + 2],
+                 in_=pair[h][:].rearrange("p (t m r) -> p r m t", t=2, r=PACK)[:, :, rows])
 
         def along_i(t, g_i, slot=None):
             gi_mx = mx_tiles("gi%d" % t, P, slot)
@@ -207,31 +207,31 @@ def tile_attend_gbpool_UV_kernel(tc, xT, dz, cf, si, U, eT, V, offs, out_0, out_
             nc.scalar.copy(out=res, in_=bank[:])
             nc.sync.dma_start(out=by_place(out_1)[:, t, :], in_=res)
 
-        g_i = sb("g_i", [P, (PACK - 1) * K], BF16)
         for t in range(2):
             gather_on_scalar(t, 0, K)
         turned = [turn(plane(t)) for t in range(2)]
-        for t in range(2):
-            copy_turned(turned[t], chunk(g_i, t))
-        first_bank = out_1_bank(along_i(0, chunk(g_i, 0)))
-        lay_pair(0, 0, nc.vector.tensor_copy)
+        g_i0 = sb("g_i0", [P, K], BF16, "table1")
+        copy_turned(turned[0], g_i0[:])
+        first_bank = out_1_bank(along_i(0, g_i0[:]))
         gather_on_vector(2, 0, VECTOR_SHARE)
         gather_on_scalar(2, VECTOR_SHARE, K)
-        store_out_1(0, first_bank, at(TABLE2_AT + 8 * K, "res1_0", [P, K], F32)[:])
-        gi1_mx = at(TABLE2_AT, "gi1_codes", [P, P], U32), sb("gi1_scales", [P, P], U8)
-        quantize(gi1_mx, E4M3, chunk(g_i, 1))
-        g_e.append(at(TABLE2_AT + 2 * K, "g_e1", [P, 2 * K], BF16))
-        lay_pair(0, 1, nc.vector.tensor_copy)
-        copy_turned(turn(plane(2)), chunk(g_i, 2))
+        g_i1 = at(TABLE2_AT, "g_i1", [P, K], BF16)
+        copy_turned(turned[1], g_i1[:])
+        store_out_1(0, first_bank, at(TABLE2_AT + 2 * K, "res1_0", [P, K], F32)[:])
+        g_e = at(TABLE2_AT + 8 * K, "g_e", [P, PACK * K], BF16)
+        lay_pair(0, 0, K, nc.vector.tensor_copy)
+        gi1_mx = along_i(1, g_i1[:])
+        g_i2 = sb("g_i2", [P, K], BF16)
+        copy_turned(turn(plane(2)), g_i2[:])
 
         gather_on_vector(3, 0, VECTOR_SHARE)
         gather_on_scalar(3, VECTOR_SHARE, K)
         last_turned = turn(plane(3))
-        gi2_mx = along_i(2, chunk(g_i, 2), "table3")
+        lay_pair(1, 0, VECTOR_SHARE, nc.vector.tensor_copy)
+        lay_pair(1, VECTOR_SHARE, K, nc.vector.tensor_copy)
+        gi2_mx = along_i(2, g_i2[:], "table3")
         second_bank = out_1_bank(gi1_mx)
         late_banks = [out_1_bank(gi2_mx)]
-        for a in range(2):
-            lay_pair(1, a, nc.vector.tensor_copy)
 
         v_b = [sb("v_b%d" % c, [P, K], BF16)[:] for c in range(PACK)]
         round_panel(v_b[0], v_raw[0][:], nc.scalar.copy)
@@ -243,10 +243,10 @@ def tile_attend_gbpool_UV_kernel(tc, xT, dz, cf, si, U, eT, V, offs, out_0, out_
         round_panel(v_b[3], v_raw[3][:], nc.scalar.copy)
 
         ge_pairs = [mx_tiles("ge01", HALF), (at(0, "ge23_codes", [P, HALF], U32), sb("ge23_scales", [P, HALF], U8))]
-        quantize(ge_pairs[0], E4M3, g_e[0][:])
+        quantize(ge_pairs[0], E4M3, chunk(g_e, 0, 2))
         first_panel = project("v0", v_b[0], ge_pairs)
         for r in range(2, PACK):
-            quantize(ge_pairs[1], E4M3, chunk(g_e[1], r - 2), (r - 2) * P)
+            quantize(ge_pairs[1], E4M3, chunk(g_e, r), (r - 2) * P)
         v_banks = [first_panel()]
         v_banks.append(project("v1", v_b[1], ge_pairs)())
         late_banks.append(out_1_bank(along_i(3, g_i3[:])))

from contextlib import ExitStack

import concourse.mybir as mybir

F32 = mybir.dt.float32
BF16 = mybir.dt.bfloat16
U32 = mybir.dt.uint32
U16 = mybir.dt.uint16
U8 = mybir.dt.uint8
E4M3 = mybir.dt.float8_e4m3fn_x4
E5M2 = mybir.dt.float8_e5m2_x4
ALU = mybir.AluOpType
COPY = mybir.ActivationFunctionType.Copy

P = 128
PACK = 4
K = 512
HALF = K // 2
QUADRANT = 32
VECTOR_SHARE = 256
TABLE2_AT = 4096
V_AT = {0: 0, 2: 16384, 3: 24576}
FLOPS = 4 * 2 * K * K * K


def tile_attend_gbpool_UV_kernel(tc, xT, dz, cf, si, U, eT, V, offs, out_0, out_1):
    nc = tc.nc
    with ExitStack() as ctx:
        keep = ctx.enter_context(tc.tile_pool(name="keep", bufs=1))
        laid = ctx.enter_context(tc.tile_pool(name="laid", bufs=1))
        psum = ctx.enter_context(tc.psum_pool(name="psum", bufs=8))

        def sb(name, shape, dtype, slot=None):
            return keep.tile(shape, dtype, name=name, tag=slot or name, align_bytes=64)

        def at(offset, name, shape, dtype):
            return laid.tile(shape, dtype, name=name, align_bytes=64, offset=offset)

        def new_bank(shape):
            return psum.tile(shape, F32, name="bank")

        def chunk(ap, c, n=1):
            return ap[:, c * K:(c + n) * K]

        def by_place(dram):
            return dram.rearrange("(p t) c -> p t c", t=PACK)

        def load(tile, src):
            nc.sync.dma_start(out=tile[:], in_=src)
            return tile

        def fetch(name, src):
            return load(sb(name, src.shape, F32), src)

        factors = sb("factors", [P, K], F32)
        nc.vector.memset(factors[:], 0.0)
        x_raw = [fetch("x_raw0", by_place(xT)[:, 0:2, :])]
        nc.sync.dma_start(out=factors[0:1, :], in_=si[0:1, :])
        nc.sync.dma_start(out=factors[1:2, :], in_=cf.rearrange("f o -> o f"))
        x_raw.append(fetch("x_raw1", by_place(xT)[:, 2:PACK, :]))
        dz_raw = fetch("dz_raw", by_place(dz))
        u_raw = fetch("u_raw", by_place(U))
        offsets = keep.tile([P, K // 16], U16, name="offsets")
        nc.sync.dma_start(offsets[:], offs)
        table = [fetch("table%d" % t, by_place(eT)[:, t, :]) if t != 2 else
                 load(at(TABLE2_AT, "table2", [P, 4 * K], F32), by_place(eT)[:, t, :]) for t in range(PACK)]
        v_raw = [load(at(V_AT[c], "v_raw%d" % c, [P, PACK, P], F32) if c in V_AT else sb("v_raw%d" % c, [P, PACK, P], F32),
                      by_place(V)[:, :, c * P:(c + 1) * P]) for c in range(PACK)]

        ones = sb("ones", [P, P], F32)
        nc.vector.memset(ones[:], 1.0)
        ramp = sb("ramp", [P, P], F32)
        nc.vector.tensor_tensor_scan(out=ramp[:], data0=ones[:], data1=ones[:], initial=-1.0, op0=ALU.mult, op1=ALU.add)
        ramp_turned = sb("ramp_turned", [P, P], F32)
        nc.vector.transpose(out=ramp_turned[:], in_=ramp[:])
        ident = sb("ident", [P, P], F32)
        for q in range(0, P, QUADRANT):
            rows = slice(q, q + QUADRANT)
            nc.vector.tensor_scalar(out=ident[rows, :], in0=ramp[rows, :], scalar1=ramp_turned[rows, q:q + 1],
                                    scalar2=None, op0=ALU.is_equal)

        factor_bank = new_bank([P, PACK, P])
        for r in range(PACK):
            nc.tensor.transpose(factor_bank[:, r, :], factors[:, r:K:PACK], ident[:])
        factor_cols = sb("factor_cols", [P, PACK, 2], F32)
        nc.scalar.copy(out=factor_cols[:], in_=factor_bank[:, :, 0:2])

        def mx_tiles(name, width, slot=None):
            return sb(name + "_codes", [P, width], U32, slot), sb(name + "_scales", [P, width], U8)

        def quantize(mx, fmt, src, first=0):
            cols = slice(first, first + src.shape[1] // PACK)
            nc.vector.quantize_mx(out=mx[0][:, cols].bitcast(fmt), scales=mx[1][:, cols], in_=src)

        def product(out, still, still_first, moving, moving_cols, fmt):
            cols = slice(still_first, still_first + P)
            nc.tensor.matmul_mx(out=out, lhsT=still[0][:, cols].bitcast(E4M3), lhsT_scale=still[1][:, cols],
                                rhs=moving[0][:, moving_cols].bitcast(fmt), rhs_scale=moving[1][:, moving_cols],
                                start=True, stop=True)

        def round_panel(dst, src, copy):
            copy(out=dst.rearrange("p (a b t) -> p a t b", b=4, t=PACK), in_=src.rearrange("p t (a b) -> p a t b", b=4))

        def project(name, rounded, pairs, slot=None):
            panel = mx_tiles(name, P, slot)
            quantize(panel, E4M3, rounded)
            return lambda: projected(panel, pairs)

        def projected(panel, pairs):
            bank = new_bank([P, PACK, P])
            for r in range(PACK):
                product(bank[:, r, :], pairs[r // 2], r % 2 * P, panel, slice(0, P), E4M3)
            return bank

        def weigh(bank, c, dst):
            nc.vector.tensor_tensor(out=dst.rearrange("p (a b r) -> p a r b", b=4, r=PACK),
                                    in0=bank[:].rearrange("p r (a b) -> p a r b", b=4),
                                    in1=weight[:, :, c * P:(c + 1) * P].rearrange("p r (a b) -> p a r b", b=4),
                                    op=ALU.mult)

        def turn(src):
            n = src.shape[1] // K
            words = src.bitcast(F32)
            bank = new_bank([P, 2 * n, P])
            for e in range(n):
                for u in range(2):
                    nc.tensor.transpose(bank[:, 2 * e + u, :], words[:, 2 * P * e + u:2 * P * (e + 1):2], ident[:])
            return bank

        def copy_turned(bank, dst):
            nc.scalar.copy(out=dst.bitcast(F32).rearrange("p (e n u) -> p e n u", n=P, u=2),
                           in_=bank[:].rearrange("p (e u) n -> p e n u", u=2))

        x_b = sb("x_b", [P, PACK * K], BF16)
        x_i = sb("x_i", [P, PACK * K], BF16)
        for h in range(2):
            nc.vector.tensor_copy(out=chunk(x_b, 2 * h, 2), in_=x_raw[h][:].rearrange("p t c -> p (t c)"))
            copy_turned(turn(chunk(x_b, 2 * h, 2)), chunk(x_i, 2 * h, 2))
        x_d = sb("x_d", [P, PACK * K], BF16)
        nc.vector.tensor_copy(out=x_d[:].rearrange("p (r m t) -> p m t r", r=PACK, t=PACK),
                              in_=x_b[:].rearrange("p (t m r) -> p m t r", t=PACK, r=PACK))

        scaled = sb("scaled", [P, PACK * K], F32)
        weight = sb("weight", [P, PACK * K], F32)[:].rearrange("p (r c) -> p r c", r=PACK)
        for j in range(PACK):
            dealt = chunk(scaled, j).rearrange("p (r m) -> p m r", r=PACK)
            row = dz_raw[:, j, :].rearrange("p (m r) -> p m r", r=PACK)
            if j < 2:
                nc.vector.tensor_scalar(out=dealt, in0=row, scalar1=factor_cols[:, j, 1:2], scalar2=None, op0=ALU.mult)
            else:
                nc.scalar.activation(out=dealt, in_=row, func=COPY, scale=factor_cols[:, j, 1:2])
        for r in range(PACK):
            bank = new_bank([P, PACK, P])
            for j in range(PACK):
                nc.tensor.transpose(bank[:, j, :], chunk(scaled, j)[:, r * P:(r + 1) * P], ident[:])
            nc.scalar.activation(out=weight[:, r, :].rearrange("p (n j) -> p n j", j=PACK),
                                 in_=bank[:].rearrange("p j n -> p n j"), func=COPY, scale=factor_cols[:, r, 0:1])

        xd_mx = mx_tiles("xd", K)
        quantize(xd_mx, E4M3, x_d[:])
        xd_pairs = [[part[:, h * HALF:(h + 1) * HALF] for part in xd_mx] for h in range(2)]
        xi_mx = mx_tiles("xi", K, "dz_raw")
        quantize(xi_mx, E4M3, x_i[:])

        u_b = sb("u_b", [P, PACK * K], BF16)
        u_banks = []
        round_panel(chunk(u_b, 0), u_raw[:, :, 0:P], nc.vector.tensor_copy)
        for c in range(PACK):
            if c + 1 < PACK:
                round_panel(chunk(u_b, c + 1), u_raw[:, :, (c + 1) * P:(c + 2) * P], nc.vector.tensor_copy)
            u_banks.append(project("u%d" % c, chunk(u_b, c), xd_pairs)())
        dv_b = sb("dv_b", [P, PACK * K], BF16)
        for c in range(PACK):
            weigh(u_banks[c], c, chunk(dv_b, c))
        dv_mx = mx_tiles("dv", K)
        for h in range(2):
            quantize(dv_mx, E5M2, chunk(dv_b, 2 * h, 2), h * HALF)

        pair = [sb("pair%d" % h, [P, 2 * K], BF16) for h in range(2)]

        def plane(t):
            return chunk(pair[t // 2], t % 2)

        def gather_on_vector(t, first, last):
            nc.vector.tensor_copy(plane(t)[:, first:last], table[t][:].indirect(offsets[:, first // 16:last // 16]))

        def gather_on_scalar(t, first, last):
            nc.scalar.activation(out=plane(t)[:, first:last],
                                 in_=table[t][:].indirect(offsets[:, first // 16:last // 16]), func=COPY)

        def lay_pair(h, first, last, copy):
            rows = slice(first // PACK, last // PACK)
            copy(out=g_e[:].rearrange("p (r m t) -> p r m t", r=PACK, t=PACK)[:, :, rows, 2 * h:2 * h + 2],
                 in_=pair[h][:].rearrange("p (t m r) -> p r m t", t=2, r=PACK)[:, :, rows])

        def along_i(t, g_i, slot=None):
            gi_mx = mx_tiles("gi%d" % t, P, slot)
            quantize(gi_mx, E4M3, g_i)
            return gi_mx

        def out_1_bank(gi_mx):
            bank = new_bank([P, K])
            product(bank[:], gi_mx, 0, dv_mx, slice(0, K), E5M2)
            return bank

        def store_out_1(t, bank, res):
            nc.scalar.copy(out=res, in_=bank[:])
            nc.sync.dma_start(out=by_place(out_1)[:, t, :], in_=res)

        for t in range(2):
            gather_on_scalar(t, 0, K)
        turned = [turn(plane(t)) for t in range(2)]
        g_i0 = sb("g_i0", [P, K], BF16, "table1")
        copy_turned(turned[0], g_i0[:])
        first_bank = out_1_bank(along_i(0, g_i0[:]))
        gather_on_vector(2, 0, VECTOR_SHARE)
        gather_on_scalar(2, VECTOR_SHARE, K)
        g_i1 = at(TABLE2_AT, "g_i1", [P, K], BF16)
        copy_turned(turned[1], g_i1[:])
        store_out_1(0, first_bank, at(TABLE2_AT + 2 * K, "res1_0", [P, K], F32)[:])
        g_e = at(TABLE2_AT + 8 * K, "g_e", [P, PACK * K], BF16)
        lay_pair(0, 0, K, nc.vector.tensor_copy)
        gi1_mx = along_i(1, g_i1[:])
        g_i2 = sb("g_i2", [P, K], BF16)
        copy_turned(turn(plane(2)), g_i2[:])

        gather_on_vector(3, 0, VECTOR_SHARE)
        gather_on_scalar(3, VECTOR_SHARE, K)
        last_turned = turn(plane(3))
        lay_pair(1, 0, VECTOR_SHARE, nc.vector.tensor_copy)
        lay_pair(1, VECTOR_SHARE, K, nc.vector.tensor_copy)
        gi2_mx = along_i(2, g_i2[:], "table3")
        second_bank = out_1_bank(gi1_mx)
        late_banks = [out_1_bank(gi2_mx)]

        v_b = [sb("v_b%d" % c, [P, K], BF16)[:] for c in range(PACK)]
        round_panel(v_b[0], v_raw[0][:], nc.scalar.copy)
        g_i3 = at(V_AT[0] + 2 * K, "g_i3", [P, K], BF16)
        copy_turned(last_turned, g_i3[:])
        for c in range(1, 3):
            round_panel(v_b[c], v_raw[c][:], nc.scalar.copy)
        store_out_1(1, second_bank, at(V_AT[2] + 2 * K, "res1_1", [P, K], F32)[:])
        round_panel(v_b[3], v_raw[3][:], nc.scalar.copy)

        ge_pairs = [mx_tiles("ge01", HALF), (at(0, "ge23_codes", [P, HALF], U32), sb("ge23_scales", [P, HALF], U8))]
        quantize(ge_pairs[0], E4M3, chunk(g_e, 0, 2))
        first_panel = project("v0", v_b[0], ge_pairs)
        for r in range(2, PACK):
            quantize(ge_pairs[1], E4M3, chunk(g_e, r), (r - 2) * P)
        v_banks = [first_panel()]
        v_banks.append(project("v1", v_b[1], ge_pairs)())
        late_banks.append(out_1_bank(along_i(3, g_i3[:])))
        v_banks.append(project("v2", v_b[2], ge_pairs)())
        du_b = [at(V_AT[2] - 2 * K, "du_b0", [P, 2 * K], BF16), at(V_AT[3] - 3 * K, "du_b1", [P, 2 * K], BF16)]
        for c in range(2):
            weigh(v_banks[c], c, chunk(du_b[0], c))
        late_res = at(V_AT[3] + 2 * K, "res1_23", [P, 2, K], F32)
        for e in range(2):
            store_out_1(2 + e, late_banks[e], late_res[:, e, :])
        v_banks.append(project("v3", v_b[3], ge_pairs)())
        du_mx = sb("du_codes", [P, K], U32), at(V_AT[3] + K, "du_scales", [P, K], U8)
        for c in range(2):
            quantize(du_mx, E5M2, chunk(du_b[0], c), c * P)
        for c in range(2, PACK):
            weigh(v_banks[c], c, chunk(du_b[1], c - 2))
        for c in range(2, PACK):
            quantize(du_mx, E5M2, chunk(du_b[1], c - 2), c * P)
        for h in range(2):
            cols = slice(h * HALF, (h + 1) * HALF)
            for t in range(PACK):
                bank = new_bank([P, HALF])
                product(bank[:], xi_mx, t * P, du_mx, cols, E5M2)
                res = sb("res0_%d_%d" % (h, t), [P, HALF], F32)
                copy = nc.vector.tensor_copy if h == 1 and t % 2 == 0 else nc.scalar.copy
                copy(out=res[:], in_=bank[:])
                nc.sync.dma_start(out=by_place(out_0)[:, t, cols], in_=res[:])
